import numpy as np, ml_dtypes
CORES = [23,119,17,113]
N = 4
import mx_ref
BF = ml_dtypes.bfloat16
def entries(a):
    return np.ascontiguousarray(a.T).reshape(-1)
def table(e):
    return np.ascontiguousarray(np.reshape(e, (-1, 16)).T).astype(np.int32)
def gentries(a):
    return np.ascontiguousarray(a.reshape(8, 16, -1).transpose(0, 2, 1)).reshape(8, -1)
def gtable(e):
    e = np.asarray(e); return np.ascontiguousarray(e.reshape(8, -1, 16).transpose(0, 2, 1)).reshape(128, -1).astype(np.int32)
def tile(rs):
    return np.stack(rs, axis=2).reshape(128, -1).astype(BF)
def pick(q, e):
    c = np.concatenate([q[0].reshape(128, -1, 4), np.zeros((128, 1, 4), np.uint8)], axis=1); s = np.concatenate([q[1], np.ones((16, 1), np.uint8)], axis=1)
    return (np.ascontiguousarray(c[:, e].reshape(128, -1)), np.ascontiguousarray(s[:, e]))
def join(*qs):
    return (np.concatenate([q[0] for q in qs], axis=1), np.concatenate([q[1] for q in qs], axis=1))
def put(q, e, v):
    c, s = q[0].reshape(128, -1, 4).copy(), q[1].copy(); c[:, e] = v[0].reshape(128, -1, 4); s[:, e] = v[1]
    return (c.reshape(128, -1), s)
def pk(c, s):
    return (np.ascontiguousarray(c), mx_ref.live(s))
def emit(q):
    return q[0], q[1]
def packed(v, rng):
    q = [mx_ref.quantize(np.ascontiguousarray(v[r])) for r in range(N)]
    return np.stack([a for a, b in q]), np.stack([mx_ref.plane(b, rng) for a, b in q])
def values_of_codes():
    e, c = np.zeros((128, 128, 4), np.float32), np.zeros((128, 2, 4), np.uint8)
    e[np.arange(128), np.arange(128), 0] = 1
    c[:127, :, 0] = np.arange(256).reshape(2, 128).T[:127]
    return mx_ref.matmul(mx_ref.quantize(e.reshape(128, 512).astype(BF)), (c.reshape(128, 8), np.full((16, 2), 127, np.uint8))).T.reshape(-1).astype(np.float64)
CODE_VALUE, SCALE_VALUE = values_of_codes(), 2.0 ** (np.arange(256) - 127.0)
def decode(q):
    return (CODE_VALUE[q[0]].reshape(16, 8, -1, 4) * SCALE_VALUE[q[1]][:, None, :, None] + 0.0).reshape(128, -1).astype(np.float32)
def f(rng, *shape):
    return mx_ref.flush((rng.standard_normal(shape, dtype=np.float32) * np.exp2(rng.integers(-2, 3, shape[:-1] + (1,)))).astype(BF))
def wide(rng, *shape, cols=0):
    v = rng.standard_normal(shape, dtype=np.float32) * np.exp2(rng.integers(-12, 13, shape)).astype(np.float32)
    if cols: v *= np.repeat(np.exp2(rng.integers(-cols, cols + 1, shape[:-2] + (1, shape[-1] // 4))) * (rng.random(shape[:-2] + (1, shape[-1] // 4)) > 0.0625), 4, axis=-1).astype(np.float32)
    return mx_ref.flush(v.astype(BF))
C, T, K, STEPS = 480, 384, 192, 3
MATES = [1, 2, 3]
DECIDE = [16 * i + k for i in range(STEPS) for k in range(2)]
def numbers_of(rng):
    return {"x": np.array(f(rng, N, 128, 4 * C)), "u": np.array(f(rng, N, 128, 512)), "v": np.array(f(rng, N, 128, 512))}
def lists(rng):
    return {"p": np.stack([gtable(np.stack([rng.permutation(C) for g in range(8)])) for r in range(N)]),
            "ln": np.stack([table(np.concatenate([rng.permutation(T) for i in range(STEPS)])) for r in range(N)])}
def layers(rng):
    k = np.exp2(rng.permuted(np.tile(np.arange(128) % 5 - 2.0, (N, 1)), axis=1))[:, :, None]
    return np.array(mx_ref.flush((rng.standard_normal((N, 128, 2048)) * k).astype(np.float32).astype(BF))).reshape(N, 8, 16, 4, 8, 16, 4)
def weights(rng, w):
    c, s = packed(np.ascontiguousarray(w).reshape(N, 128, 2048), rng)
    return {"wc": c, "ws": s}
def setup_inputs(rng):
    return {**numbers_of(rng), **lists(rng), **weights(rng, layers(rng))}
def setup_inputs_ties(rng):
    d = numbers_of(rng)
    x = d["x"].reshape(N, 8, 16, C, 4)
    x[:, :, 0] = 0
    x[:, :, 0, :, 0] = rng.integers(-1, 2, (N, 8, C)).astype(np.float32).astype(BF)
    x[:, :, :, ::8] = 0
    u = d["u"].reshape(N, 128, 128, 4)
    u[:, :, DECIDE] = 0
    o = rng.permutation(N)
    for r in range(N):
        g = rng.permutation(8)
        for i, c in enumerate(DECIDE): u[r, 16 * g[i], c, 0] = 0.0 if r == o[0] else -1.0 if r == o[1] else 1.0
    w = layers(rng)
    w[:, :, 0] = 0
    w[:, :, :, :, :, 0] = 0
    return {"x": x.reshape(N, 128, 4 * C), "u": u.reshape(N, 128, 512), "v": d["v"], **lists(rng), **weights(rng, w)}
def setup_inputs_near(rng):
    d = numbers_of(rng)
    x = d["x"].reshape(N, 8, 16, C, 4)
    u = d["u"].reshape(N, 128, 128, 4)
    x[:, :, :8] = 0
    u[:, :, DECIDE] = 0
    o = rng.permutation(N)
    for r in range(N):
        k = 2.0 ** -30 if o[r] % 2 == 0 else 1.0
        s = rng.integers(-1, 2, (8, C)) * k
        x[r, :, 0, :, 0] = (1.125 * s).astype(np.float32).astype(BF)
        x[r, :, 1, :, 0] = (-s).astype(np.float32).astype(BF)
        for g in rng.permutation(8)[:4]:
            c = rng.integers(T)
            x[r, g, 0, c, 0] = 2.0 ** 16 * rng.choice([-1.0, 1.0])
            x[r, g, 1, c, 0] = 0
        g = rng.permutation(8)
        for i, c in enumerate(DECIDE):
            u[r, 16 * g[i], c, 0] = 1.125 * k
            u[r, 16 * g[i] + 1, c, 0] = 1.25 * k
    w = layers(rng)
    w[:, :, :8] = 0
    w[:, :, :, :, :, :8] = 0
    return {"x": x.reshape(N, 128, 4 * C), "u": u.reshape(N, 128, 512), "v": d["v"], **lists(rng), **weights(rng, w)}
def setup_inputs_twice(rng):
    d = numbers_of(rng)
    x = d["x"].reshape(N, 8, 16, C, 4)
    a = (2 * rng.integers(2, 8, (N, 8, 8, C, 4)) + 1) * np.exp2(rng.integers(-5, -3, (N, 8, 8, C, 4)))
    a[:, :, 0, :, 0] = 1.96875 * 2.0 ** 12
    x[:, :, :8] = (a * rng.choice([-1.0, 1.0], a.shape)).astype(np.float32).astype(BF)
    w = layers(rng)
    w[:, :, 0] = 0
    w[:, :, :, :, :, :8] = 0
    return {"x": x.reshape(N, 128, 4 * C), "u": d["u"], "v": d["v"], **lists(rng), **weights(rng, w)}
def setup_inputs_ends(rng):
    d = numbers_of(rng)
    e = rng.permutation(N) % 4
    x, w = np.zeros((N, 8, 16, C, 4)), np.zeros((N, 128, 4, 128, 4), np.float32)
    u = d["u"].reshape(N, 128, 128, 4)
    v, p, n, j, i = [], [], [], np.arange(C), np.arange(128)
    for r in range(N):
        k = e[r]
        s = rng.choice([-1.0, 1.0], (8, 1, C, 1))
        x[r] = 2.0 ** 17 * (1.0, s[:1], 2.0 ** -47, s)[k]
        for c in DECIDE:
            a = (2.0 ** 30, 0.0, 2.0 ** -30 if c % 16 else -2.0 ** -30, 2.0 ** 30 * rng.choice([-1.0, 1.0], (128, 4)))[k]
            u[r, :, c] = np.asarray(a, np.float32).astype(BF)
        v.append((1.0 if k == 0 else rng.choice([-1.0, 1.0], (128, 512))) * np.full((128, 512), 2.0 ** (-30 if k == 2 else 30)))
        if k == 3:
            for b in range(4): w[r, (i + 16) % 128, b, i, b] = -1024
        else: w[r] = (2, 0, -2)[k]
        p.append(gtable((np.tile(j, (8, 1)), np.tile(j[::-1], (8, 1)), (j + 16 * np.arange(8)[:, None] + 1) % C, np.stack([rng.permutation(C) for g in range(8)]))[k]))
        n.append(table((np.tile(np.arange(T), STEPS), np.tile(np.arange(T)[::-1], STEPS), np.tile(rng.permutation(T), STEPS), np.concatenate([rng.permutation(T) for g in range(STEPS)]))[k]))
    return {"x": x.astype(np.float32).reshape(N, 128, 4 * C).astype(BF), "u": u.reshape(N, 128, 512), "v": np.stack(v).astype(np.float32).astype(BF), "p": np.stack(p), "ln": np.stack(n), **weights(rng, w.astype(BF))}
def setup_inputs_spread(rng):
    d = setup_inputs(rng)
    d["x"] = wide(rng, N, 128, 4 * C, cols=2)
    return d
def check_inputs(d):
    b = []
    for k, most in (("x", 2.0 ** 17), ("u", 2.0 ** 30), ("v", 2.0 ** 30)):
        a = np.abs(d[k].astype(np.float32))
        if not (np.isfinite(a).all() and ((a == 0) | (a >= 2.0 ** -30) & (a <= most)).all()): b.append("a value of " + k)
    none, least, most = [emit(mx_ref.quantize(np.full((128, 16), k, np.float32).astype(BF)))[1][0, 0] for k in (0.0, 2.0 ** -30, 2.0 ** 30)]
    for r in range(N):
        if (np.sort(gentries(d["p"][r]), axis=1) != np.arange(C)).any(): b.append("p: a group's entries aren't a permutation")
        if (np.sort(entries(d["ln"][r]).reshape(STEPS, T), axis=1) != np.arange(T)).any(): b.append("ln: a step's entries aren't a permutation")
        if ((d["wc"][r] & 0x7F) == 0x7F).any(): b.append("wc: a code that is no number")
        s = mx_ref.live(d["ws"][r])
        if ((s != none) & ((s < least) | (s > most))).any(): b.append("ws: a scale out of range")
        with np.errstate(all="ignore"):
            w = np.abs(decode(pk(d["wc"][r], d["ws"][r]))).astype(np.float64).reshape(128, 512, 4)
            if not np.max(np.sum(w, axis=(0, 2))) <= 1024: b.append("W: the sizes of a column add up to more than 1024")
    return b
def moves(s, p, ln):
    at = C * np.arange(8)[:, None] + p
    has = at.copy()
    for i in range(STEPS):
        link = 2 * ln[T * i:T * i + T] + (s[16 * i + 1] > 0)
        push, stack, own = s[16 * i] > 0, has[:, :T].copy(), has[link % 8, T + link // 8]
        has[:, :T] = np.where(push, np.concatenate([own[None], stack[:7]]), np.concatenate([stack[1:], own[None]]))
        has[link % 8, T + link // 8] = np.where(push, stack[7], stack[0])
    m = np.zeros(8 * C, np.int64)
    m[at] = has
    return m
def moved(t, m):
    z = t.reshape(8, 16, C, 4).transpose(0, 2, 1, 3).reshape(8 * C, 16, 4)[m]
    return np.ascontiguousarray(z.reshape(8, C, 16, 4).transpose(0, 2, 1, 3)).reshape(128, 4 * C)
def reference(x, u, v, p, ln, wc, ws):
    qu = [mx_ref.quantize(u[r]) for r in range(N)]
    lay = [pk(wc[r], ws[r]) for r in range(N)]
    now = [x[r] for r in range(N)]
    for a in MATES:
        m, qz = [], []
        for r in range(N):
            s = mx_ref.matmul(qu[r], mx_ref.quantize(np.ascontiguousarray(now[r][:, :4 * T])))
            m.append(moves(s, gentries(p[r]), entries(ln[r])))
            qz.append(mx_ref.quantize(moved(now[r], m[r])))
        for r in range(N):
            h = join(pick(qz[r ^ a], np.arange(K)), pick(qz[r], np.arange(K, C)))
            has = decode(h)
            made = tile([np.maximum(mx_ref.matmul(pick(lay[r], np.arange(128 * b, 128 * b + 128)), h), np.float32(0.0)) * np.float32(0.015625) + has[:, b::4] for b in range(4)])
            now[r] = moved(made, np.argsort(m[r]))
    y, op = np.zeros((N, 128, C), np.float32), np.zeros((N, 8, C), np.float32)
    oc, osc = np.zeros((N, 128, 4 * C), np.uint8), np.zeros((N, 16, C), np.uint8)
    for r in range(N):
        q = mx_ref.quantize(now[r])
        y[r] = mx_ref.matmul(mx_ref.quantize(v[r]), q)
        op[r] = m[r].reshape(8, C)
        oc[r], osc[r] = emit(q)
    return {"y": y, "op": op, "oc": oc, "osc": osc}

@@ -1,0 +1,516 @@
+from concourse.mybir import dt, AluOpType, AxisListType, ActivationFunctionType
+
+A = AluOpType
+OPS = {"+": A.add, "-": A.subtract, "*": A.mult, "&": A.bitwise_and, ">>": A.logical_shift_right, "=": A.is_equal, "!=": A.not_equal, "<": A.is_lt, ">=": A.is_ge, ">": A.is_gt}
+MATES = (1, 2, 3)
+C, KX = 480, 192
+BLK = 2048
+
+SCRATCH, POOL = {}, {}
+for _d, _l in (("bfloat16", "xin 1920 xt 1920 zt 1920 yw 16384 ut 512 vt 512 zpad 512 ones 512 e0 512 e1 512 e2 512 ew 2048 eb 2048 ed 2048 idt 128 bwF 384 bwB 384 bt 1536 n16 1536"),
+               ("int32", "pi 30 li 72 pid 8"),
+               ("float32", "ji 480 j5 384 psi 480 mk 1536 rs1 1536 i1 384 i3 384 r2 384 r3 384 l2h 384 src 384 fb 1536 fm 1536 scn 1536 loc0 4096 loc1 4096 loc2 4096 fr 480 frb 480 opw 3840 opo 480 rb0 288 rb1 288 rb2 288 rb3 288 yo 480")):
+    _l = _l.split()
+    for _k in range(0, len(_l), 2):
+        SCRATCH[_l[_k]] = ("sbuf", [128, int(_l[_k + 1])], _d)
+for _b, _d, _l in (
+        ("wi", "int32", "lcd 24 lcF 24 lcB 24 qli 6 sgi 96 bli 96 blm 96 tb 72 tlo 72 thi 72 lnn 90 l3 90 l4 90 cv 96 p1 96 p2 60 p3 30 b1 36 b2 30 b3 6 qq 90 v21 24 v20 24 idi 30 idm 30"),
+        ("wf", "float32", "qlf 6 sgf 96 jst 24 l5 90 t96F 96 t96B 96 t90F 90 t90B 90 kp 96 kt 30 actt 30 pt 96 qt 90 ss 30 m90 90 mb 30 ov 30 md 6 dd 6 df 90 ee 30"),
+        ("wu", "uint16", "pu 30 lu 72 lcuF 24 lcuB 24 qlu 6 sgu 96 plu 30 bluF 96 bluB 96 uluF 8 uluB 8 fluF 30 fluB 30 zlu 30 xlu 30"),
+        ("cs", "float32", "sc 32 k16 16 oh 8 ohq 16 cf 32 pr 16 ulf 8")):
+    _l, _o = _l.split(), 0
+    for _k in range(0, len(_l), 2):
+        POOL[_l[_k]] = (_b, _o)
+        _o += (int(_l[_k + 1]) + 15) // 16 * 16
+    SCRATCH[_b] = ("sbuf", [128, _o], _d)
+for _n, _w in (("u", 128), ("uF", 128), ("uB", 128), ("v", 128), ("w", 512), ("e", 512), ("d", 512), ("x", 480), ("z", 480), ("b", 512),
+               ("l0", KX), ("l1", KX), ("l2", KX)):
+    SCRATCH["q" + _n] = ("sbuf", [128, _w], "float8_e4m3fn_x4")
+    SCRATCH["s" + _n] = ("sbuf", [128, _w], "uint8")
+BANKS = ["bank%d" % _k for _k in range(8)]
+for _n in BANKS:
+    SCRATCH[_n] = ("psum", [128, 512], "float32")
+SEMAPHORES = ["e_v", "e_a", "e_t", "e_g"] + ["d%d" % _k for _k in range(30)] + ["rc%d" % _k for _k in range(3)] + ["ls%d" % _k for _k in range(3)]
+
+
+def rank_program(g, core, T, topo):
+    rank = T.rank_of(core)
+    if rank is None:
+        return
+    ENG = {"v": g.vector, "a": g.scalar, "t": g.tensor, "g": g, "s": g.sync}
+    cnt, seen, hist, nb = {}, {q: {} for q in ENG}, {}, [0]
+
+    def R(name, c0, c1, step=1, p0=0, p1=128):
+        if name in POOL:
+            name, o = POOL[name]
+            c0, c1 = c0 + o, c1 + o
+        ap = T[name][p0:p1, c0:c1] if step == 1 else T[name][p0:p1, c0:c1:step]
+        if name in BANKS:
+            return ap, [(name, 0, 512, (1, 0), 0, 128)]
+        return ap, [(name, c0, c1, (step, c0 % step), p0, p1)]
+
+    def ind(win, off):
+        return win[0].indirect(off[0]), win[1] + off[1]
+
+    def codes(name, c0, c1, d=None):
+        ap = T[name][:, c0:c1]
+        return (ap if d is None else ap.bitcast(d)), [(name, c0, c1, (1, 0), 0, 128)]
+
+    def emit(q, fn, reads, writes, tok=None):
+        dma, need, new = tok is not None, {}, []
+        for isw, regs in ((False, reads), (True, writes)):
+            for (name, c0, c1, ph, p0, p1) in regs:
+                for h in hist.get(name, ()):
+                    if h[1] <= c0 or c1 <= h[0] or h[4] <= p0 or p1 <= h[3]:
+                        continue
+                    if h[2][0] == ph[0] and h[2][1] != ph[1]:
+                        continue
+                    if q == "t" and h[6] == q and isw:
+                        continue
+                    if not (isw or h[5] or (name in BANKS and h[6] != q)):
+                        continue
+                    if dma and tok[0] == h[7]:
+                        continue
+                    need[h[7]] = max(need.get(h[7], 0), h[8])
+                new.append((name, c0, c1, ph, p0, p1, isw))
+        for s in need:
+            if seen[q].get(s, 0) < need[s]:
+                ENG[q].wait_ge(T.sem[s], need[s])
+                seen[q][s] = need[s]
+        ins = fn()
+        if not dma:
+            s = "e_" + q
+            cnt[s] = cnt.get(s, 0) + 1
+            ins.then_inc(T.sem[s], 1)
+            tok = (s, cnt[s])
+        for (name, c0, c1, ph, p0, p1, isw) in new:
+            old = hist.get(name, [])
+            if isw and ph[0] == 1:
+                old = [h for h in old if not (c0 <= h[0] and h[1] <= c1 and p0 <= h[3] and h[4] <= p1)]
+            elif not isw and not dma:
+                old = [h for h in old if h[5] or h[9] or h[6] != q or h[:5] != (c0, c1, ph, p0, p1)]
+            hist[name] = old + [(c0, c1, ph, p0, p1, isw, q, tok[0], tok[1], dma)]
+
+    def sr(*xs):
+        r = []
+        for x in xs:
+            if isinstance(x, tuple):
+                r = r + x[1]
+        return r
+
+    def ap(x):
+        return x[0] if isinstance(x, tuple) else x
+
+    def col(k):
+        return R("sc", k, k + 1)
+
+    def tt(o, a, b, op):
+        emit("v", lambda: g.vector.tensor_tensor(o[0], a[0], b[0], op), sr(a, b), o[1])
+
+    def ts(o, a, s1, s2, op0, op1=None):
+        if op1 is None:
+            emit("v", lambda: g.vector.tensor_scalar(o[0], a[0], ap(s1), None, op0), sr(a, s1), o[1])
+        else:
+            emit("v", lambda: g.vector.tensor_scalar(o[0], a[0], ap(s1), ap(s2), op0, op1), sr(a, s1, s2), o[1])
+
+    def cp(o, a):
+        emit("v", lambda: g.vector.tensor_copy(o[0], a[0]), a[1], o[1])
+
+    def fill(o, val):
+        emit("v", lambda: g.vector.memset(o[0], val), [], o[1])
+
+    def opd(w):
+        if w[0] == "#":
+            return col(int(w[1:]))
+        if ":" in w:
+            n, k = w.split(":")[0], [int(z) for z in w.split(":")[1:]]
+            return R(n, *k)
+        return float(w) if "." in w else int(w)
+
+    def X(text, m=""):
+        for ln in text.replace("$", m).split("\n"):
+            w = ln.split()
+            if not w:
+                continue
+            o, a = opd(w[0]), opd(w[1])
+            if len(w) == 2:
+                (cp if isinstance(a, tuple) else fill)(o, a)
+            elif len(w) == 4 and ":" in w[3]:
+                tt(o, a, opd(w[3]), OPS[w[2]])
+            elif len(w) == 4:
+                ts(o, a, opd(w[3]), None, OPS[w[2]])
+            else:
+                ts(o, a, opd(w[3]), opd(w[5]), OPS[w[2]], OPS[w[4]])
+
+    def scatter(dst, n, off, src):
+        w, i = ind(R(dst, 0, n), off), R(src, 0, n)
+        emit("v", lambda: g.vector.tensor_copy(w[0], i[0]), i[1] + off[1], R(dst, 0, n)[1])
+
+    def act(o, a, func="Copy", scale=1.0):
+        if func == "Copy":
+            emit("a", lambda: g.scalar.activation(o[0], a[0], ActivationFunctionType.Copy), a[1], o[1])
+        else:
+            f = ActivationFunctionType.Relu if func == "Relu" else ActivationFunctionType.Identity
+            emit("a", lambda: g.scalar.activation(o[0], a[0], f, scale=ap(scale)), sr(a, scale), o[1])
+
+    def quant(x, c0, c1, tile, t0=0):
+        q, s, i = codes("q" + x, c0, c1), R("s" + x, c0, c1), R(tile, t0, t0 + 4 * (c1 - c0))
+        emit("v", lambda: g.vector.quantize_mx(q[0], s[0], i[0]), i[1], q[1] + s[1])
+
+    def mm(bank, n, a, a0, b, b0, start=True, stop=True):
+        o, la, sa, lb, sb = R(BANKS[bank], 0, n), codes("q" + a, a0, a0 + 128), R("s" + a, a0, a0 + 128), codes("q" + b, b0, b0 + n), R("s" + b, b0, b0 + n)
+        emit("t", lambda: g.tensor.matmul_mx(o[0], la[0], sa[0], lb[0], sb[0], start, stop), sr(la, sa, lb, sb), o[1])
+
+    def iota(o, pat, fl=True, cm=0):
+        if fl:
+            emit("g", lambda: g.iota(o[0], pat, 0, cm, allow_small_or_imprecise_dtypes=True), [], o[1])
+        else:
+            emit("g", lambda: g.iota(o[0], pat, 0, cm), [], o[1])
+
+    def asel(o, a, pat, op, base, cm):
+        emit("g", lambda: g.affine_select(o[0], a[0], pat, op, 0.0, base, cm), a[1], o[1])
+
+    def dmas(items):
+        s, tot = "d%d" % nb[0], 16 * len(items)
+        nb[0] += 1
+        cnt[s] = tot
+        for q, o, i in items:
+            emit(q, lambda: ENG[q].dma_start(o[0], i[0]).then_inc(T.sem[s], 16), i[1], o[1], (s, tot))
+
+    def ext(a):
+        return a, []
+
+    def scan(n, src, s0=0):
+        o, d0, d1 = R("scn", s0, n), R("rs1", s0, n), R(src, s0, n)
+        emit("v", lambda: g.vector.tensor_tensor_scan(o[0], d0[0], d1[0], 0.0, A.mult, A.add), sr(d0, d1), o[1])
+
+    def rotate(name, blk, c0, c1, qs):
+        it = []
+        for k in range(1, 8):
+            e = 128 - 16 * k
+            it.append((blk * k, 0, e, 16 * k, 128))
+            it.append((blk * k, e, 128, 0, 16 * k))
+        dmas([(qs[n % len(qs)], R(name, o + c0, o + c1, 1, a, b), R(name, c0, c1, 1, d, e)) for n, (o, a, b, d, e) in enumerate(it)])
+
+    dmas([("s" if k % 2 else "a", R("li", 0, 72, 1, 16 * k, 16 * k + 16), ext(T.ln[:, :])) for k in range(8)])
+    dmas([("s", R("xin", 0, 1920), ext(T.x[:, :]))])
+    dmas([("a", R("pi", 0, 30), ext(T.p[:, :])), ("a", R("ut", 0, 512), ext(T.u[:, :]))])
+
+    iota(R("pid", 0, 1), [[1, 1]], False, 1)
+    iota(R("k16", 0, 16), [[1, 16]])
+    iota(R("ji", 0, 480), [[1, 480]])
+    iota(R("psi", 0, 480), [[384, 5], [1, 96]])
+    iota(R("qli", 0, 6), [[64, 6]], False)
+    iota(R("sgi", 0, 96), [[4, 4], [64, 24]], False)
+    iota(R("jst", 0, 24), [[16, 24]])
+    iota(R("n16", 0, 1536), [[0, 96], [1, 16]])
+    X("""ones:0:512 1.0
+    pid:1:2 pid:0:1 & 15
+    pid:2:3 pid:0:1 >> 4
+    pid:3:4 pid:0:1 >> 2 & 3
+    pid:4:5 pid:0:1 & 3
+    pid:5:6 pid:0:1 >> 4 & 1
+    pid:6:7 pid:0:1 >> 5
+    pid:7:8 pid:0:1 & 1
+    #0 pid:1:2
+    #1 pid:2:3
+    #3 pid:2:3 * -512.0
+    #4 pid:2:3 * -2048.0
+    #5 pid:2:3 * 2048.0
+    #6 pid:5:6
+    #2 pid:3:4 * 16.0
+    #19 pid:1:2 * 4.0
+    #16 pid:6:7
+    oh:0:8 k16:0:8 = #1
+    ohq:0:16 k16:0:16 = #0
+    cf:0:32 0.0
+    #2 sc:2:3 + pid:4:5
+    #14 #3 + 384.0
+    #10 oh:0:1 + oh:7:8
+    #19 sc:19:20 + sc:16:17""")
+
+    LOF = {1: 0, 2: 24, 3: 48}
+
+    def lst(i, buf="lu"):
+        return R(buf, LOF[i], LOF[i] + 24)
+
+    X("lu:0:72 li:0:72")
+    scatter("i1", 384, lst(1), "ji")
+    scatter("i3", 384, lst(3), "ji")
+    X("""j5:0:384 ji:0:384 * 512.0
+    pu:0:30 pi:0:30
+    loc0:480:512 0.0""")
+    for k in range(5):
+        for b in range(4):
+            act(R("yw", 384 * k + 96 * b, 384 * k + 96 * b + 96), R("xin", 384 * k + b, 384 * k + 384, 4))
+    rotate("yw", BLK, 0, 1920, "s")
+    ts(R("loc0", 0, 480), ind(R("psi", 0, 480), R("pu", 0, 30)), col(5), None, A.add)
+    rotate("loc0", 512, 0, 512, "s")
+    dmas([("s", codes("qw", 0, 512, dt.uint8), ext(T.wc[:, :])), ("s", R("sw", 0, 512), ext(T.ws[:, :]))])
+    dmas([("s", R("vt", 0, 512), ext(T.v[:, :]))])
+    act(R("l2h", 0, 384), ind(R("j5", 0, 384), lst(2)))
+    X("""qlf:0:6 qli:0:6 + #19
+    sgf:0:96 sgi:0:96 + #2
+    jst:0:24 jst:0:24 + #0 + 1536.0
+    qlu:0:6 qlf:0:6
+    sgu:0:96 sgf:0:96
+    mk:0:1536 n16:0:1536 = #0
+    rs1:0:1536 n16:0:1536 > 0.0""")
+
+    asel(R("e0", 0, 512), R("ones", 0, 512), [[0, 32], [1, 4], [-1, 4]], A.is_equal, 0, 0)
+    asel(R("e1", 0, 512), R("e0", 0, 512), [[16, 8], [0, 64]], A.is_ge, 15, -1)
+    asel(R("e2", 0, 512), R("e1", 0, 512), [[-16, 8], [0, 64]], A.is_ge, 0, 1)
+    for w in range(4):
+        asel(R("ew", 512 * w, 512 * w + 512), R("e2", 0, 512), [[0, 8], [1, 4], [0, 16]], A.is_equal, -w, 0)
+    asel(R("idt", 0, 128), R("ones", 0, 128), [[-1, 128]], A.is_equal, 0, 1)
+    iota(R("opw", 0, 3840), [[1, 3840]])
+
+    def prepare(m, a1, a2, a3, v1, v3):
+        tt(R("src", 0, 384), ind(R("j5", 0, 384), lst(a1)), R("ji", 0, 384), A.add)
+        scatter("r2", 384, lst(a2), "src")
+        tt(R("src", 0, 384), ind(R(v1, 0, 384), lst(a2)), R("l2h", 0, 384), A.add)
+        scatter("r3", 384, lst(a3), "src")
+        tt(R("lcd", 0, 24), lst(a3, "li"), lst(a2, "li"), A.subtract)
+        X("lcd:0:24 lcd:0:24 * #10")
+        tt(R("lc" + m, 0, 24), R("lcd", 0, 24), lst(a2, "li"), A.add)
+        X("lcu$:0:24 lc$:0:24", m)
+        ql = R("qlu", 0, 6)
+        segs = [(384, 480, v3, ql), (480, 864, "r2", lst(a3)), (864, 960, "r2", ql),
+                (960, 1344, v1, R("lcu" + m, 0, 24)), (1344, 1440, v1, ql), (1440, 1536, "r3", ql)]
+        act(R("fb", 0, 384), R("ji", 0, 384))
+        for c0, c1, w, off in segs:
+            act(R("fb", c0, c1), ind(R(w, 0, 384), off))
+        for c0, c1, w, off in segs:
+            tt(R("fm", c0, c1), ind(R(w, 0, 384), off), R("mk", c0, c1), A.mult)
+        scan(1536, "fm", 384)
+        X("tb:0:72 scn:399:1536:16")
+        tt(R("fm", 0, 1536), ind(R("fb", 0, 1536), R("sgu", 0, 96)), R("mk", 0, 1536), A.mult)
+        scan(1536, "fm")
+        cp(R("lnn", 0, 24), lst(a1, "li"))
+        X("""bli:0:96 scn:15:1536:16
+        tlo:0:72 tb:0:72 & 511
+        thi:0:72 tb:0:72 >> 9
+        blm:0:96 bli:0:96 & 511
+        lnn:60:84 lc$:0:24
+        lnn:84:90 qlf:0:6
+        blu$:0:96 blm:0:96
+        t96$:0:24 jst:0:24
+        t96$:24:96 tlo:0:72 + #3
+        lnn:24:30 thi:66:72
+        lnn:30:60 thi:6:36
+        t96$:24:30 t96$:24:30 + 1024.0
+        t96$:30:60 t96$:30:60 + 512.0
+        l3:0:90 lnn:0:90 & 3
+        l4:0:90 lnn:0:90 >> 2
+        l5:0:90 l3:0:90 * 1024.0 + #14
+        t90$:0:90 l5:0:90 + l4:0:90""", m)
+
+    prepare("F", 1, 2, 3, "i1", "i3")
+    for k, x in ((0, 6), (2, 22), (5, 1), (7, 17), (8, -83), (9, -79), (14, -99), (15, -103)):
+        fill(R("cf", k, k + 1), float(x))
+    for k in range(7):
+        fill(R("cf", 16 + k, 17 + k), float(2 ** k))
+    for dst, c0, n, oh, add in ((12, 16, 16, "ohq", 0.0), (7, 0, 8, "oh", -1.0), (9, 8, 8, "oh", 99.0)):
+        o, i = col(dst), R("pr", 0, n)
+        tt(i, R(oh, 0, n), R("cf", c0, c0 + n), A.mult)
+        emit("v", lambda: g.vector.tensor_reduce(o[0], i[0], AxisListType.X, A.add), i[1], o[1])
+        if add:
+            ts(col(dst), col(dst), add, None, A.add)
+    act(R("eb", 0, 2048), R("ew", 0, 2048), "Identity", col(12))
+    X("""#8 #1 >= 4.0 * -2.0
+    sc:15:16 oh:1:2 + oh:6:7
+    #13 pid:7:8 * -1.0 + 1.0
+    pid:2:3 pid:0:1 >> 1 & 3
+    #8 #8 + 1.0
+    #11 #15 * -1.0 + 1.0
+    #13 sc:13:14 - ohq:6:7""")
+    for m, sgn, a6, a16 in (("F", "16.0 + 0.0", "-15.0", "-16.0"), ("B", "-16.0 + 32.0", "17.0", "16.0")):
+        X("""#17 pid:2:3 * %s
+        #18 ohq:6:7 * %s
+        #20 ohq:6:7 * %s
+        #17 sc:17:18 + pid:7:8
+        #17 sc:17:18 + sc:18:19
+        ulf:0:8 k16:0:8 * 0.0 + #17
+        ulf:1:2 ulf:1:2 + sc:20:21
+        ulf:6:7 ulf:6:7 + sc:20:21
+        ulu$:0:8 ulf:0:8""" % (sgn, a6, a16), m)
+    quant("u", 0, 128, "ut")
+    for m in "FB":
+        o, w = codes("qu" + m, 0, 128, dt.uint32), ind(codes("qu", 0, 128, dt.uint32), R("ulu" + m, 0, 8))
+        emit("v", lambda: g.vector.tensor_copy(o[0], w[0]), w[1], o[1])
+        cp(R("su" + m, 0, 128), ind(R("su", 0, 128), R("ulu" + m, 0, 8)))
+    quant("x", 0, 480, "xin")
+    X("""kp:0:30 -1024.0
+    kp:30:60 2560.0
+    kp:60:96 3584.0
+    kt:0:24 -1024.0
+    kt:24:30 1280.0
+    actt:0:30 1.0
+    zpad:0:512 0.0
+    ed:0:2048 0.0
+    actt:0:24 actt:0:24 * #11
+    qq:84:90 k16:0:6 * 0.0 + #6""")
+    quant("b", 384, 512, "zpad")
+    scatter("frb", 480, R("pu", 0, 30), "ji")
+    X("fm:0:480 frb:0:480 * mk:0:480")
+    scan(480, "fm")
+    X("plu:0:30 scn:15:480:16")
+    for w in range(4):
+        quant("e", 128 * w, 128 * w + 128, "eb", 512 * w)
+    for b in range(4):
+        act(R("ed", 512 * b + b, 512 * b + 512, 4), R("idt", 0, 128))
+    for k in range(8):
+        fill(R("yw", BLK * k + 1920, BLK * k + 2048), 0.0)
+    for k in (1, 2):
+        fill(R("loc%d" % k, 480, 512), 0.0)
+
+    def moves(m):
+        mm(0, 384, "u" + m, 0, "x", 0)
+        bw, s = R("bw" + m, 0, 384), R(BANKS[0], 0, 384)
+        if m == "F":
+            ts(bw, s, 0.0, None, A.is_gt)
+        else:
+            ts(bw, s, 0.0, col(13), A.is_gt, A.not_equal)
+        act(R("bt", 768, 1536), ind(bw, R("blu" + m, 48, 96)))
+        cp(R("bt", 0, 768), ind(bw, R("blu" + m, 0, 48)))
+        quant("b", 0, 384, "bt")
+        for w in range(4):
+            mm(1, 128, "e", 128 * w, "b", 96 * w, w == 0, w == 3)
+        cp(R("cv", 0, 96), R(BANKS[1], 0, 96))
+        X("""p1:0:96 cv:0:96 & 1
+        qq:0:24 cv:0:24 >> 1 & 1
+        qq:24:30 cv:24:30 >> 3 & 1
+        qq:30:60 cv:30:60 >> 1 & 1
+        qq:60:84 cv:0:24 >> 6 & 1
+        pt:0:96 p1:0:96 * kp:0:96
+        p2:0:60 cv:0:60 >> 2 & 1
+        p3:0:30 cv:0:30 >> 4 & 1
+        b1:0:36 cv:60:96 >> 1 & 1
+        qt:0:90 qq:0:90 * 512.0
+        pt:0:96 pt:0:96 + t96$:0:96
+        ss:0:30 p2:0:30 + p3:0:30
+        b2:0:30 cv:30:60 >> 3 & 1
+        qt:0:90 qt:0:90 + t90$:0:90
+        md:0:6 b1:30:36 = qq:24:30
+        ss:0:30 ss:0:30 * kt:0:30
+        v21:0:24 cv:0:24 & 21
+        dd:0:6 pt:90:96 - qt:24:30
+        pt:0:30 pt:0:30 + ss:0:30
+        m90:24:30 p2:24:30 != p3:24:30
+        dd:0:6 dd:0:6 * md:0:6
+        m90:30:60 p1:30:60 != p2:30:60
+        m90:60:90 b1:0:30 != qq:60:90
+        qt:24:30 qt:24:30 + dd:0:6
+        m90:0:24 v21:0:24 = #7
+        v20:0:24 cv:0:24 & 20
+        df:0:90 qt:0:90 - pt:0:90
+        mb:0:30 b2:0:30 = qq:60:90
+        b3:0:6 cv:24:30 >> 5 & 1
+        df:0:90 df:0:90 * m90:0:90
+        mb:0:30 mb:0:30 * actt:0:30
+        ov:0:24 v20:0:24 * #8 < #9
+        df:0:90 df:0:90 + pt:0:90
+        ov:24:30 b3:0:6 = qq:84:90
+        ee:0:30 df:30:60 - df:60:90
+        ee:0:30 ee:0:30 * mb:0:30
+        ee:0:30 ee:0:30 + df:60:90
+        df:0:30 df:0:30 - ee:0:30
+        df:0:30 df:0:30 * ov:0:30
+        idi:0:30 df:0:30 + ee:0:30
+        idm:0:30 idi:0:30 & 4095
+        flu$:0:30 idm:0:30""", m)
+
+    def pick(dst, win, width, off):
+        act(R(dst, 224, 480), ind(R(win, 0, width), R(off, 14, 30)))
+        cp(R(dst, 0, 224), ind(R(win, 0, width), R(off, 0, 14)))
+
+    def fold(src):
+        tt(R("fm", 0, 480), ind(R(src, 0, 480), R("plu", 0, 30)), R("mk", 0, 480), A.mult)
+        scan(480, "fm")
+
+    def by_column(src, dst):
+        fold(src)
+        X("idi:0:30 scn:15:480:16 + #4\nidm:0:30 idi:0:30 & %d\n%s:0:30 idm:0:30" % (8 * BLK - 1, dst))
+
+    def collect(tile, off, k0, k1):
+        for b in range(4):
+            (cp, act)[b % 2](R(tile, 64 * k0 + b, 64 * k1, 4), ind(R("yw", 96 * b, 8 * BLK), R(off, k0, k1)))
+
+    def layer(src, c0, n, i0):
+        for b in range(4):
+            mm(b, n, "w", 128 * b, src, c0)
+            mm(4 + b, n, "d", 128 * b, src, c0)
+            act(R("rb%d" % b, 0, n), R(BANKS[b], 0, n), "Relu", 0.015625)
+        for b in range(4):
+            for k in range(n // 96):
+                d = 384 * (i0 + k) + 96 * b
+                tt(R("yw", d, d + 96), R("rb%d" % b, 96 * k, 96 * k + 96), R(BANKS[4 + b], 96 * k, 96 * k + 96), A.add)
+
+    peers = [T.cores[rank ^ k] for k in MATES]
+    engs = topo.mask(core, peers[0]) & topo.mask(core, peers[1]) & topo.mask(core, peers[2])
+    ne = bin(engs).count("1")
+
+    for r in range(3):
+        last = r == 2
+        moves("F")
+        pick("fr", "loc%d" % r, 4096, "fluF")
+        by_column("fr", "zlu")
+        collect("zt", "zlu", 0, 12)
+        quant("z", 0, KX, "zt")
+        rid, pid, _se = topo.addr(peers[r])
+        for kind in "qs":
+            i = codes("qz", 0, KX, dt.uint8) if kind == "q" else R("sz", 0, KX)
+            o = codes("ql%d" % r, 0, KX, dt.uint8) if kind == "q" else R("sl%d" % r, 0, KX)
+            emit("g", lambda: g.remote_dma(o[0], i[0], T.sem["rc%d" % r], T.sem["ls%d" % r], pid, rid, engs), i[1], [], ("ls%d" % r, 2 * ne))
+            hist[kind + "l%d" % r] = [(0, KX, (1, 0), 0, 128, True, "g", "rc%d" % r, 2 * ne, True)]
+        cnt["ls%d" % r] = 2 * ne
+        cnt["rc%d" % r] = 2 * ne
+        collect("zt", "zlu", 12, 30)
+        quant("z", KX, C, "zt", 4 * KX)
+        if r == 0:
+            for b in range(4):
+                quant("d", 128 * b, 128 * b + 128, "ed", 512 * b)
+        layer("z", KX, C - KX, 2)
+        rotate("yw", BLK, 768, 1920, "s")
+        if r == 0:
+            prepare("B", 3, 2, 1, "i3", "i1")
+        else:
+            moves("B")
+        if last:
+            quant("v", 0, 128, "vt")
+            pick("fr", "loc0", 4096, "fluF")
+            fold("fr")
+            X("""cv:0:30 scn:15:480:16
+            p1:0:30 cv:0:30 >> 7 & 15
+            p2:0:30 cv:0:30 >> 11
+            p3:0:30 cv:0:30 & 2047
+            p1:30:60 p1:0:30 * 171.0
+            ee:0:30 p2:0:30 * 480.0
+            p1:60:90 p1:30:60 >> 9
+            ee:0:30 ee:0:30 + p3:0:30
+            ss:0:30 p1:60:90 * -288.0
+            ee:0:30 ee:0:30 + ss:0:30
+            zlu:0:30 ee:0:30""")
+            pick("opo", "opw", 3840, "zlu")
+            dmas([("s", ext(T.op[k:k + 1, :]), R("opo", 0, 480, 1, 16 * k, 16 * k + 1)) for k in range(8)])
+        layer("l%d" % r, 0, KX, 0)
+        rotate("yw", BLK, 0, 768, "sa")
+        if r == 0:
+            moves("B")
+        loc = "frb" if last else "loc%d" % (r + 1)
+        pick(loc, "loc0", 4096, "fluB")
+        by_column(loc, "xlu")
+        if last:
+            collect("xt", "xlu", 0, 30)
+            quant("x", 0, 480, "xt")
+            mm(0, 480, "v", 0, "x", 0)
+            act(R("yo", 0, 480), R(BANKS[0], 0, 480))
+            dmas([("s", ext(T.oc[:, :]), codes("qx", 0, 480, dt.uint8))]
+                 + [("s", ext(T.osc[4 * k:4 * k + 4, :]), R("sx", 0, 480, 1, 32 * k, 32 * k + 4)) for k in range(4)])
+            dmas([("a", ext(T.y[:, :]), R("yo", 0, 480))])
+        else:
+            rotate(loc, 512, 0, 512, "s")
+            collect("xt", "xlu", 0, 24)
+            quant("x", 0, 384, "xt")
+    for s in sorted(cnt):
+        g.wait_ge(T.sem[s], cnt[s])

@@ -3,13 +3,14 @@ from concourse.mybir import dt, AluOpType, AxisListType, ActivationFunctionType
 A = AluOpType
 OPS = {"+": A.add, "-": A.subtract, "*": A.mult, "&": A.bitwise_and, ">>": A.logical_shift_right, "=": A.is_equal, "!=": A.not_equal, "<": A.is_lt, ">=": A.is_ge, ">": A.is_gt}
 MATES = (1, 2, 3)
+WEIGHTS = (1, 512, 4, 1024, 16, 2048, 4096)
 C, KX = 480, 192
 BLK = 2048
 
 SCRATCH, POOL = {}, {}
-for _d, _l in (("bfloat16", "xin 1920 xt 1920 zt 1920 yw 16384 ut 512 vt 512 zpad 512 ones 512 e0 512 e1 512 e2 512 ew 2048 eb 2048 ed 2048 idt 128 bwF 384 bwB 384 bt 1536 n16 1536"),
+for _d, _l in (("bfloat16", "xin 1920 xt 1920 zt 1920 yw 16384 ut 512 vt 512 zpad 512 ones 512 mk 480 e0 512 e1 512 e2 512 ew 2048 eb 2048 ed 2048 bwF 384 bwB 384 bt 1536 n16 480"),
                ("int32", "pi 30 li 72 pid 8"),
-               ("float32", "ji 480 j5 384 psi 480 mk 1536 rs1 1536 i1 384 i3 384 r2 384 r3 384 l2h 384 src 384 fb 1536 fm 1536 scn 1536 loc0 4096 loc1 4096 loc2 4096 fr 480 frb 480 opw 3840 opo 480 rb0 288 rb1 288 rb2 288 rb3 288 yo 480")):
+               ("float32", "ji 480 j5 384 psi 480 tr 384 trd 384 rs1 480 i1 384 i3 384 r2F 384 r3F 384 r2B 384 r3B 384 l2h 384 src 384 fbF 1536 fbB 1536 ftF 1536 ftB 1536 fm 480 scn 480 loc0 4096 loc1 4096 loc2 4096 fr 480 frb 480 opw 3840 opo 480 rb0 288 rb1 288 rb2 288 rb3 288 yo 480")):
     _l = _l.split()
     for _k in range(0, len(_l), 2):
         SCRATCH[_l[_k]] = ("sbuf", [128, int(_l[_k + 1])], _d)
@@ -116,9 +117,6 @@ def rank_program(g, core, T, topo):
     def cp(o, a):
         emit("v", lambda: g.vector.tensor_copy(o[0], a[0]), a[1], o[1])
 
-    def fill(o, val):
-        emit("v", lambda: g.vector.memset(o[0], val), [], o[1])
-
     def opd(w):
         if w[0] == "#":
             return col(int(w[1:]))
@@ -134,7 +132,7 @@ def rank_program(g, core, T, topo):
                 continue
             o, a = opd(w[0]), opd(w[1])
             if len(w) == 2:
-                (cp if isinstance(a, tuple) else fill)(o, a)
+                cp(o, a)
             elif len(w) == 4 and ":" in w[3]:
                 tt(o, a, opd(w[3]), OPS[w[2]])
             elif len(w) == 4:
@@ -161,11 +159,14 @@ def rank_program(g, core, T, topo):
         o, la, sa, lb, sb = R(BANKS[bank], 0, n), codes("q" + a, a0, a0 + 128), R("s" + a, a0, a0 + 128), codes("q" + b, b0, b0 + n), R("s" + b, b0, b0 + n)
         emit("t", lambda: g.tensor.matmul_mx(o[0], la[0], sa[0], lb[0], sb[0], start, stop), sr(la, sa, lb, sb), o[1])
 
-    def iota(o, pat, fl=True, cm=0):
+    def iota(o, pat, fl=True, cm=0, base=0):
         if fl:
-            emit("g", lambda: g.iota(o[0], pat, 0, cm, allow_small_or_imprecise_dtypes=True), [], o[1])
+            emit("g", lambda: g.iota(o[0], pat, base, cm, allow_small_or_imprecise_dtypes=True), [], o[1])
         else:
-            emit("g", lambda: g.iota(o[0], pat, 0, cm), [], o[1])
+            emit("g", lambda: g.iota(o[0], pat, base, cm), [], o[1])
+
+    def const(name, c0, c1, val):
+        iota(R(name, c0, c1), [[0, c1 - c0]], True, 0, val)
 
     def asel(o, a, pat, op, base, cm):
         emit("g", lambda: g.affine_select(o[0], a[0], pat, op, 0.0, base, cm), a[1], o[1])
@@ -180,8 +181,16 @@ def rank_program(g, core, T, topo):
     def ext(a):
         return a, []
 
-    def scan(n, src, s0=0):
-        o, d0, d1 = R("scn", s0, n), R("rs1", s0, n), R(src, s0, n)
+    def turn(src, k0):
+        dmas([("s", R("tr", k0 + 32 * b + 16 * (k % 2), k0 + 32 * b + 16 * (k % 2) + 16, 1, 32 * (k // 2), 32 * (k // 2) + 32),
+               R(src, 512 * b, 512 * b + 512, 1, 16 * k, 16 * k + 1)) for k in range(8) for b in range(3)])
+
+    def turned(k0):
+        o, i = R("trd", k0, k0 + 96), R("tr", k0, k0 + 96)
+        emit("v", lambda: g.vector.transpose(o[0], i[0]), i[1], o[1])
+
+    def scan(n, src):
+        o, d0, d1 = R("scn", 0, n), R("rs1", 0, n), R(src, 0, n)
         emit("v", lambda: g.vector.tensor_tensor_scan(o[0], d0[0], d1[0], 0.0, A.mult, A.add), sr(d0, d1), o[1])
 
     def rotate(name, blk, c0, c1, qs):
@@ -203,9 +212,12 @@ def rank_program(g, core, T, topo):
     iota(R("qli", 0, 6), [[64, 6]], False)
     iota(R("sgi", 0, 96), [[4, 4], [64, 24]], False)
     iota(R("jst", 0, 24), [[16, 24]])
-    iota(R("n16", 0, 1536), [[0, 96], [1, 16]])
-    X("""ones:0:512 1.0
-    pid:1:2 pid:0:1 & 15
+    iota(R("n16", 0, 480), [[0, 30], [1, 16]])
+    const("cf", 0, 32, 0)
+    for k, x in ((0, 6), (2, 22), (5, 1), (7, 17), (8, -83), (9, -79), (14, -99), (15, -103)) + tuple((16 + k, WEIGHTS[k]) for k in range(7)):
+        const("cf", k, k + 1, x)
+    const("ones", 0, 512, 1)
+    X("""pid:1:2 pid:0:1 & 15
     pid:2:3 pid:0:1 >> 4
     pid:3:4 pid:0:1 >> 2 & 3
     pid:4:5 pid:0:1 & 3
@@ -223,7 +235,6 @@ def rank_program(g, core, T, topo):
     #16 pid:6:7
     oh:0:8 k16:0:8 = #1
     ohq:0:16 k16:0:16 = #0
-    cf:0:32 0.0
     #2 sc:2:3 + pid:4:5
     #14 #3 + 384.0
     #10 oh:0:1 + oh:7:8
@@ -239,58 +250,65 @@ def rank_program(g, core, T, topo):
     scatter("i3", 384, lst(3), "ji")
     X("""j5:0:384 ji:0:384 * 512.0
     pu:0:30 pi:0:30
-    loc0:480:512 0.0""")
+    mk:0:480 n16:0:480 = #0
+    rs1:0:480 n16:0:480 > 0.0""")
+    for k in range(3):
+        const("loc%d" % k, 480, 512, 0)
+    ts(R("loc0", 0, 480), ind(R("psi", 0, 480), R("pu", 0, 30)), col(5), None, A.add)
     for k in range(5):
         for b in range(4):
             act(R("yw", 384 * k + 96 * b, 384 * k + 96 * b + 96), R("xin", 384 * k + b, 384 * k + 384, 4))
-    rotate("yw", BLK, 0, 1920, "s")
-    ts(R("loc0", 0, 480), ind(R("psi", 0, 480), R("pu", 0, 30)), col(5), None, A.add)
-    rotate("loc0", 512, 0, 512, "s")
-    dmas([("s", codes("qw", 0, 512, dt.uint8), ext(T.wc[:, :])), ("s", R("sw", 0, 512), ext(T.ws[:, :]))])
-    dmas([("s", R("vt", 0, 512), ext(T.v[:, :]))])
     act(R("l2h", 0, 384), ind(R("j5", 0, 384), lst(2)))
     X("""qlf:0:6 qli:0:6 + #19
     sgf:0:96 sgi:0:96 + #2
     jst:0:24 jst:0:24 + #0 + 1536.0
     qlu:0:6 qlf:0:6
-    sgu:0:96 sgf:0:96
-    mk:0:1536 n16:0:1536 = #0
-    rs1:0:1536 n16:0:1536 > 0.0""")
+    sgu:0:96 sgf:0:96""")
 
     asel(R("e0", 0, 512), R("ones", 0, 512), [[0, 32], [1, 4], [-1, 4]], A.is_equal, 0, 0)
     asel(R("e1", 0, 512), R("e0", 0, 512), [[16, 8], [0, 64]], A.is_ge, 15, -1)
     asel(R("e2", 0, 512), R("e1", 0, 512), [[-16, 8], [0, 64]], A.is_ge, 0, 1)
     for w in range(4):
         asel(R("ew", 512 * w, 512 * w + 512), R("e2", 0, 512), [[0, 8], [1, 4], [0, 16]], A.is_equal, -w, 0)
-    asel(R("idt", 0, 128), R("ones", 0, 128), [[-1, 128]], A.is_equal, 0, 1)
+    const("zpad", 0, 512, 0)
+    for c0, c1, x in ((0, 30, -1024), (30, 60, 2560), (60, 96, 3584)):
+        const("kp", c0, c1, x)
+    const("kt", 0, 24, -1024)
+    const("kt", 24, 30, 1280)
+    const("actt", 0, 30, 1)
+    for k in range(8):
+        const("yw", BLK * k + 1920, BLK * k + 2048, 0)
+    for b in range(4):
+        asel(R("ed", 512 * b, 512 * b + 512), R("ones", 0, 512), [[1, 512]], A.is_equal, -b, -4)
     iota(R("opw", 0, 3840), [[1, 3840]])
 
-    def prepare(m, a1, a2, a3, v1, v3):
+    def prepare(m, a1, a2, a3, v1, v3, k0):
         tt(R("src", 0, 384), ind(R("j5", 0, 384), lst(a1)), R("ji", 0, 384), A.add)
-        scatter("r2", 384, lst(a2), "src")
+        scatter("r2" + m, 384, lst(a2), "src")
         tt(R("src", 0, 384), ind(R(v1, 0, 384), lst(a2)), R("l2h", 0, 384), A.add)
-        scatter("r3", 384, lst(a3), "src")
+        scatter("r3" + m, 384, lst(a3), "src")
         tt(R("lcd", 0, 24), lst(a3, "li"), lst(a2, "li"), A.subtract)
         X("lcd:0:24 lcd:0:24 * #10")
         tt(R("lc" + m, 0, 24), R("lcd", 0, 24), lst(a2, "li"), A.add)
         X("lcu$:0:24 lc$:0:24", m)
-        ql = R("qlu", 0, 6)
-        segs = [(384, 480, v3, ql), (480, 864, "r2", lst(a3)), (864, 960, "r2", ql),
-                (960, 1344, v1, R("lcu" + m, 0, 24)), (1344, 1440, v1, ql), (1440, 1536, "r3", ql)]
-        act(R("fb", 0, 384), R("ji", 0, 384))
-        for c0, c1, w, off in segs:
-            act(R("fb", c0, c1), ind(R(w, 0, 384), off))
-        for c0, c1, w, off in segs:
-            tt(R("fm", c0, c1), ind(R(w, 0, 384), off), R("mk", c0, c1), A.mult)
-        scan(1536, "fm", 384)
-        X("tb:0:72 scn:399:1536:16")
-        tt(R("fm", 0, 1536), ind(R("fb", 0, 1536), R("sgu", 0, 96)), R("mk", 0, 1536), A.mult)
-        scan(1536, "fm")
+        ql, fb = R("qlu", 0, 6), "fb" + m
+        act(R(fb, 0, 384), R("ji", 0, 384))
+        for c0, c1, w, off in ((384, 480, v3, ql), (480, 864, "r2" + m, lst(a3)), (864, 960, "r2" + m, ql),
+                               (960, 1344, v1, R("lcu" + m, 0, 24)), (1344, 1440, v1, ql), (1440, 1536, "r3" + m, ql)):
+            act(R(fb, c0, c1), ind(R(w, 0, 384), off))
+        act(R("ft" + m, 0, 1536), ind(R(fb, 0, 1536), R("sgu", 0, 96)))
+        turn("ft" + m, k0)
+        turn(fb, k0 + 96)
+
+    def tables(m, a1, k0):
+        turned(k0)
+        X("bli:0:96 trd:%d:%d" % (k0, k0 + 96))
+        turned(k0 + 96)
+        X("tb:0:72 trd:%d:%d" % (k0 + 120, k0 + 192))
         cp(R("lnn", 0, 24), lst(a1, "li"))
-        X("""bli:0:96 scn:15:1536:16
+        X("""blm:0:96 bli:0:96 & 511
         tlo:0:72 tb:0:72 & 511
         thi:0:72 tb:0:72 >> 9
-        blm:0:96 bli:0:96 & 511
         lnn:60:84 lc$:0:24
         lnn:84:90 qlf:0:6
         blu$:0:96 blm:0:96
@@ -305,11 +323,12 @@ def rank_program(g, core, T, topo):
         l5:0:90 l3:0:90 * 1024.0 + #14
         t90$:0:90 l5:0:90 + l4:0:90""", m)
 
-    prepare("F", 1, 2, 3, "i1", "i3")
-    for k, x in ((0, 6), (2, 22), (5, 1), (7, 17), (8, -83), (9, -79), (14, -99), (15, -103)):
-        fill(R("cf", k, k + 1), float(x))
-    for k in range(7):
-        fill(R("cf", 16 + k, 17 + k), float(2 ** k))
+    prepare("F", 1, 2, 3, "i1", "i3", 0)
+    rotate("yw", BLK, 0, 1920, "s")
+    rotate("loc0", 512, 0, 512, "s")
+    dmas([("s", codes("qw", 0, 512, dt.uint8), ext(T.wc[:, :])), ("s", R("sw", 0, 512), ext(T.ws[:, :]))])
+    dmas([("s", R("vt", 0, 512), ext(T.v[:, :]))])
+    prepare("B", 3, 2, 1, "i3", "i1", 192)
     for dst, c0, n, oh, add in ((12, 16, 16, "ohq", 0.0), (7, 0, 8, "oh", -1.0), (9, 8, 8, "oh", 99.0)):
         o, i = col(dst), R("pr", 0, n)
         tt(i, R(oh, 0, n), R("cf", c0, c0 + n), A.mult)
@@ -339,32 +358,20 @@ def rank_program(g, core, T, topo):
         o, w = codes("qu" + m, 0, 128, dt.uint32), ind(codes("qu", 0, 128, dt.uint32), R("ulu" + m, 0, 8))
         emit("v", lambda: g.vector.tensor_copy(o[0], w[0]), w[1], o[1])
         cp(R("su" + m, 0, 128), ind(R("su", 0, 128), R("ulu" + m, 0, 8)))
-    quant("x", 0, 480, "xin")
-    X("""kp:0:30 -1024.0
-    kp:30:60 2560.0
-    kp:60:96 3584.0
-    kt:0:24 -1024.0
-    kt:24:30 1280.0
-    actt:0:30 1.0
-    zpad:0:512 0.0
-    ed:0:2048 0.0
-    actt:0:24 actt:0:24 * #11
-    qq:84:90 k16:0:6 * 0.0 + #6""")
+    quant("x", 0, 384, "xin")
+    X("""actt:0:24 actt:0:24 * #11
+    qq:84:90 k16:0:6 * 0.0 + #6
+    qq:84:90 qq:84:90 * 512.0""")
     quant("b", 384, 512, "zpad")
     scatter("frb", 480, R("pu", 0, 30), "ji")
     X("fm:0:480 frb:0:480 * mk:0:480")
     scan(480, "fm")
     X("plu:0:30 scn:15:480:16")
+    tables("F", 1, 0)
     for w in range(4):
         quant("e", 128 * w, 128 * w + 128, "eb", 512 * w)
-    for b in range(4):
-        act(R("ed", 512 * b + b, 512 * b + 512, 4), R("idt", 0, 128))
-    for k in range(8):
-        fill(R("yw", BLK * k + 1920, BLK * k + 2048), 0.0)
-    for k in (1, 2):
-        fill(R("loc%d" % k, 480, 512), 0.0)
 
-    def moves(m):
+    def bits(m):
         mm(0, 384, "u" + m, 0, "x", 0)
         bw, s = R("bw" + m, 0, 384), R(BANKS[0], 0, 384)
         if m == "F":
@@ -377,40 +384,41 @@ def rank_program(g, core, T, topo):
         for w in range(4):
             mm(1, 128, "e", 128 * w, "b", 96 * w, w == 0, w == 3)
         cp(R("cv", 0, 96), R(BANKS[1], 0, 96))
+
+    def origins(m):
         X("""p1:0:96 cv:0:96 & 1
-        qq:0:24 cv:0:24 >> 1 & 1
-        qq:24:30 cv:24:30 >> 3 & 1
-        qq:30:60 cv:30:60 >> 1 & 1
-        qq:60:84 cv:0:24 >> 6 & 1
+        qq:0:24 cv:0:24 & 512
+        qq:24:30 cv:24:30 >> 1 & 512
+        qq:30:60 cv:30:60 & 512
+        qq:60:84 cv:0:24 >> 3 & 512
         pt:0:96 p1:0:96 * kp:0:96
         p2:0:60 cv:0:60 >> 2 & 1
         p3:0:30 cv:0:30 >> 4 & 1
-        b1:0:36 cv:60:96 >> 1 & 1
-        qt:0:90 qq:0:90 * 512.0
+        b1:0:36 cv:60:96 & 512
+        qt:0:90 qq:0:90 + t90$:0:90
         pt:0:96 pt:0:96 + t96$:0:96
         ss:0:30 p2:0:30 + p3:0:30
-        b2:0:30 cv:30:60 >> 3 & 1
-        qt:0:90 qt:0:90 + t90$:0:90
+        b2:0:30 cv:30:60 >> 1 & 512
         md:0:6 b1:30:36 = qq:24:30
-        ss:0:30 ss:0:30 * kt:0:30
         v21:0:24 cv:0:24 & 21
+        ss:0:30 ss:0:30 * kt:0:30
         dd:0:6 pt:90:96 - qt:24:30
-        pt:0:30 pt:0:30 + ss:0:30
         m90:24:30 p2:24:30 != p3:24:30
-        dd:0:6 dd:0:6 * md:0:6
         m90:30:60 p1:30:60 != p2:30:60
+        pt:0:30 pt:0:30 + ss:0:30
+        dd:0:6 dd:0:6 * md:0:6
         m90:60:90 b1:0:30 != qq:60:90
-        qt:24:30 qt:24:30 + dd:0:6
         m90:0:24 v21:0:24 = #7
+        qt:24:30 qt:24:30 + dd:0:6
         v20:0:24 cv:0:24 & 20
+        b3:0:6 cv:24:30 >> 2 & 512
         df:0:90 qt:0:90 - pt:0:90
         mb:0:30 b2:0:30 = qq:60:90
-        b3:0:6 cv:24:30 >> 5 & 1
+        ov:24:30 b3:0:6 = qq:84:90
         df:0:90 df:0:90 * m90:0:90
         mb:0:30 mb:0:30 * actt:0:30
         ov:0:24 v20:0:24 * #8 < #9
         df:0:90 df:0:90 + pt:0:90
-        ov:24:30 b3:0:6 = qq:84:90
         ee:0:30 df:30:60 - df:60:90
         ee:0:30 ee:0:30 * mb:0:30
         ee:0:30 ee:0:30 + df:60:90
@@ -452,7 +460,8 @@ def rank_program(g, core, T, topo):
 
     for r in range(3):
         last = r == 2
-        moves("F")
+        bits("F")
+        origins("F")
         pick("fr", "loc%d" % r, 4096, "fluF")
         by_column("fr", "zlu")
         collect("zt", "zlu", 0, 12)
@@ -472,12 +481,26 @@ def rank_program(g, core, T, topo):
                 quant("d", 128 * b, 128 * b + 128, "ed", 512 * b)
         layer("z", KX, C - KX, 2)
         rotate("yw", BLK, 768, 1920, "s")
+        if r > 0:
+            bits("B")
+        layer("l%d" % r, 0, KX, 0)
+        rotate("yw", BLK, 0, 768, "sa")
         if r == 0:
-            prepare("B", 3, 2, 1, "i3", "i1")
-        else:
-            moves("B")
+            tables("B", 3, 192)
+            bits("B")
+        origins("B")
+        loc = "frb" if last else "loc%d" % (r + 1)
+        pick(loc, "loc0", 4096, "fluB")
+        by_column(loc, "xlu")
         if last:
             quant("v", 0, 128, "vt")
+            collect("xt", "xlu", 0, 30)
+            quant("x", 0, 480, "xt")
+            mm(0, 480, "v", 0, "x", 0)
+            act(R("yo", 0, 480), R(BANKS[0], 0, 480))
+            dmas([("s", ext(T.oc[:, :]), codes("qx", 0, 480, dt.uint8))]
+                 + [("s", ext(T.osc[4 * k:4 * k + 4, :]), R("sx", 0, 480, 1, 32 * k, 32 * k + 4)) for k in range(4)])
+            dmas([("a", ext(T.y[:, :]), R("yo", 0, 480))])
             pick("fr", "loc0", 4096, "fluF")
             fold("fr")
             X("""cv:0:30 scn:15:480:16
@@ -493,21 +516,6 @@ def rank_program(g, core, T, topo):
             zlu:0:30 ee:0:30""")
             pick("opo", "opw", 3840, "zlu")
             dmas([("s", ext(T.op[k:k + 1, :]), R("opo", 0, 480, 1, 16 * k, 16 * k + 1)) for k in range(8)])
-        layer("l%d" % r, 0, KX, 0)
-        rotate("yw", BLK, 0, 768, "sa")
-        if r == 0:
-            moves("B")
-        loc = "frb" if last else "loc%d" % (r + 1)
-        pick(loc, "loc0", 4096, "fluB")
-        by_column(loc, "xlu")
-        if last:
-            collect("xt", "xlu", 0, 30)
-            quant("x", 0, 480, "xt")
-            mm(0, 480, "v", 0, "x", 0)
-            act(R("yo", 0, 480), R(BANKS[0], 0, 480))
-            dmas([("s", ext(T.oc[:, :]), codes("qx", 0, 480, dt.uint8))]
-                 + [("s", ext(T.osc[4 * k:4 * k + 4, :]), R("sx", 0, 480, 1, 32 * k, 32 * k + 4)) for k in range(4)])
-            dmas([("a", ext(T.y[:, :]), R("yo", 0, 480))])
         else:
             rotate(loc, 512, 0, 512, "s")
             collect("xt", "xlu", 0, 24)

@@ -8,30 +8,30 @@ C, KX = 480, 192
 BLK = 2048
 
 SCRATCH, POOL = {}, {}
-for _d, _l in (("bfloat16", "xin 1920 xt 1920 zt 1920 yw 16384 ut 512 vt 512 zpad 512 ones 512 mk 480 e0 512 e1 512 e2 512 ew 2048 eb 2048 ed 2048 bwF 384 bwB 384 bt 1536 n16 480"),
+for _d, _l in (("bfloat16", "xin 1920 xt 1920 zt 1920 yw 16384 ut 512 vt 512 zpad 512 ones 512 mk 480 e0 512 e1 512 e2 512 ew 2048 eb 2048 ed 2048 bw 384 bt 1536 n16 480"),
                ("int32", "pi 30 li 72 pid 8"),
-               ("float32", "ji 480 j5 384 psi 480 tr 384 trd 384 rs1 480 i1 384 i3 384 r2F 384 r3F 384 r2B 384 r3B 384 l2h 384 src 384 fbF 1536 fbB 1536 ftF 1536 ftB 1536 fm 480 scn 480 loc0 4096 loc1 4096 loc2 4096 fr 480 frb 480 opw 3840 opo 480 rb0 288 rb1 288 rb2 288 rb3 288 yo 480")):
+               ("float32", "ji 480 j5 384 psi 480 tr 192 trd 192 rs1 480 i1 384 i3 384 r2 384 r3 384 l2h 384 src 384 fb 1536 ft 1536 fm 480 scn 480 loc0 4096 loc1 4096 loc2 4096 loc3 4096 fr 480 frb 480 opw 3840 opo 480 rb0 288 rb1 288 rb2 288 rb3 288 yo 480")):
     _l = _l.split()
     for _k in range(0, len(_l), 2):
         SCRATCH[_l[_k]] = ("sbuf", [128, int(_l[_k + 1])], _d)
 for _b, _d, _l in (
-        ("wi", "int32", "lcd 24 lcF 24 lcB 24 qli 6 sgi 96 bli 96 blm 96 tb 72 tlo 72 thi 72 lnn 90 l3 90 l4 90 cv 96 p1 96 p2 60 p3 30 b1 36 b2 30 b3 6 qq 90 v21 24 v20 24 idi 30 idm 30"),
-        ("wf", "float32", "qlf 6 sgf 96 jst 24 l5 90 t96F 96 t96B 96 t90F 90 t90B 90 kp 96 kt 30 actt 30 pt 96 qt 90 ss 30 m90 90 mb 30 ov 30 md 6 dd 6 df 90 ee 30"),
-        ("wu", "uint16", "pu 30 lu 72 lcuF 24 lcuB 24 qlu 6 sgu 96 plu 30 bluF 96 bluB 96 uluF 8 uluB 8 fluF 30 fluB 30 zlu 30 xlu 30"),
+        ("wi", "int32", "lcd 24 lc 24 qli 6 sgi 96 bli 96 blm 96 tb 72 tlo 72 thi 72 lnn 90 l3 90 l4 90 cv 96 p1 96 p2 60 p3 30 b1 36 b2 30 b3 6 qq 90 v21 24 v20 24 idi 30 idm 30"),
+        ("wf", "float32", "qlf 6 sgf 96 jst 24 l5 90 t96 96 t90 90 kp 96 kt 30 actt 30 pt 96 qt 90 ss 30 m90 90 mb 30 ov 30 md 6 dd 6 df 90 ee 30"),
+        ("wu", "uint16", "pu 30 lu 72 lcu 24 qlu 6 sgu 96 plu 30 blu 96 ulu 8 flu 30 zlu 30 xlu 30"),
         ("cs", "float32", "sc 32 k16 16 oh 8 ohq 16 cf 32 pr 16 ulf 8")):
     _l, _o = _l.split(), 0
     for _k in range(0, len(_l), 2):
         POOL[_l[_k]] = (_b, _o)
         _o += (int(_l[_k + 1]) + 15) // 16 * 16
     SCRATCH[_b] = ("sbuf", [128, _o], _d)
-for _n, _w in (("u", 128), ("uF", 128), ("uB", 128), ("v", 128), ("w", 512), ("e", 512), ("d", 512), ("x", 480), ("z", 480), ("b", 512),
+for _n, _w in (("u", 128), ("up", 128), ("v", 128), ("w", 512), ("e", 512), ("d", 512), ("x", 480), ("z", 480), ("b", 512),
                ("l0", KX), ("l1", KX), ("l2", KX)):
     SCRATCH["q" + _n] = ("sbuf", [128, _w], "float8_e4m3fn_x4")
     SCRATCH["s" + _n] = ("sbuf", [128, _w], "uint8")
 BANKS = ["bank%d" % _k for _k in range(8)]
 for _n in BANKS:
     SCRATCH[_n] = ("psum", [128, 512], "float32")
-SEMAPHORES = ["e_v", "e_a", "e_t", "e_g"] + ["d%d" % _k for _k in range(30)] + ["rc%d" % _k for _k in range(3)] + ["ls%d" % _k for _k in range(3)]
+SEMAPHORES = ["e_v", "e_a", "e_t", "e_g"] + ["d%d" % _k for _k in range(34)] + ["rc%d" % _k for _k in range(3)] + ["ls%d" % _k for _k in range(3)]
 
 
 def rank_program(g, core, T, topo):
@@ -125,8 +125,8 @@ def rank_program(g, core, T, topo):
             return R(n, *k)
         return float(w) if "." in w else int(w)
 
-    def X(text, m=""):
-        for ln in text.replace("$", m).split("\n"):
+    def X(text):
+        for ln in text.split("\n"):
             w = ln.split()
             if not w:
                 continue
@@ -140,8 +140,8 @@ def rank_program(g, core, T, topo):
             else:
                 ts(o, a, opd(w[3]), opd(w[5]), OPS[w[2]], OPS[w[4]])
 
-    def scatter(dst, n, off, src):
-        w, i = ind(R(dst, 0, n), off), R(src, 0, n)
+    def scatter(dst, n, off, i):
+        w = ind(R(dst, 0, n), off)
         emit("v", lambda: g.vector.tensor_copy(w[0], i[0]), i[1] + off[1], R(dst, 0, n)[1])
 
     def act(o, a, func="Copy", scale=1.0):
@@ -171,12 +171,16 @@ def rank_program(g, core, T, topo):
     def asel(o, a, pat, op, base, cm):
         emit("g", lambda: g.affine_select(o[0], a[0], pat, op, 0.0, base, cm), a[1], o[1])
 
-    def dmas(items):
-        s, tot = "d%d" % nb[0], 16 * len(items)
+    def batch(n):
+        s = "d%d" % nb[0]
         nb[0] += 1
-        cnt[s] = tot
+        cnt[s] = 16 * n
+        return s, 16 * n
+
+    def dmas(items):
+        t = batch(len(items))
         for q, o, i in items:
-            emit(q, lambda: ENG[q].dma_start(o[0], i[0]).then_inc(T.sem[s], 16), i[1], o[1], (s, tot))
+            emit(q, lambda: ENG[q].dma_start(o[0], i[0]).then_inc(T.sem[t[0]], 16), i[1], o[1], t)
 
     def ext(a):
         return a, []
@@ -201,6 +205,12 @@ def rank_program(g, core, T, topo):
             it.append((blk * k, e, 128, 0, 16 * k))
         dmas([(qs[n % len(qs)], R(name, o + c0, o + c1, 1, a, b), R(name, c0, c1, 1, d, e)) for n, (o, a, b, d, e) in enumerate(it)])
 
+    def gather_home(name, s):
+        t, w, e = batch(2), 512 * s, 128 - 16 * s
+        for a, b, c, d in ((16 * s, 128, 0, e), (0, 16 * s, e, 128)):
+            o, i = R(name, 0, w, 1, a, b), R(name, w, 2 * w, 1, c, d)
+            emit("g", lambda: g.dma_start(o[0], i[0], accum_op=A.add).then_inc(T.sem[t[0]], 16), i[1], o[1], t)
+
     dmas([("s" if k % 2 else "a", R("li", 0, 72, 1, 16 * k, 16 * k + 16), ext(T.ln[:, :])) for k in range(8)])
     dmas([("s", R("xin", 0, 1920), ext(T.x[:, :]))])
     dmas([("a", R("pi", 0, 30), ext(T.p[:, :])), ("a", R("ut", 0, 512), ext(T.u[:, :]))])
@@ -217,6 +227,12 @@ def rank_program(g, core, T, topo):
     for k, x in ((0, 6), (2, 22), (5, 1), (7, 17), (8, -83), (9, -79), (14, -99), (15, -103)) + tuple((16 + k, WEIGHTS[k]) for k in range(7)):
         const("cf", k, k + 1, x)
     const("ones", 0, 512, 1)
+    const("zpad", 0, 512, 0)
+    for c0, c1, x in ((0, 30, -1024), (30, 60, 2560), (60, 96, 3584)):
+        const("kp", c0, c1, x)
+    const("kt", 0, 24, -1024)
+    const("kt", 24, 30, 1280)
+    const("actt", 0, 30, 1)
     X("""pid:1:2 pid:0:1 & 15
     pid:2:3 pid:0:1 >> 4
     pid:3:4 pid:0:1 >> 2 & 3
@@ -240,20 +256,18 @@ def rank_program(g, core, T, topo):
     #10 oh:0:1 + oh:7:8
     #19 sc:19:20 + sc:16:17""")
 
-    LOF = {1: 0, 2: 24, 3: 48}
-
     def lst(i, buf="lu"):
-        return R(buf, LOF[i], LOF[i] + 24)
+        return R(buf, 24 * i - 24, 24 * i)
 
+    JI = R("ji", 0, 384)
     X("lu:0:72 li:0:72")
-    scatter("i1", 384, lst(1), "ji")
-    scatter("i3", 384, lst(3), "ji")
+    scatter("i1", 384, lst(1), JI)
+    scatter("i3", 384, lst(3), JI)
     X("""j5:0:384 ji:0:384 * 512.0
     pu:0:30 pi:0:30
     mk:0:480 n16:0:480 = #0
     rs1:0:480 n16:0:480 > 0.0""")
-    for k in range(3):
-        const("loc%d" % k, 480, 512, 0)
+    const("loc0", 480, 512, 0)
     ts(R("loc0", 0, 480), ind(R("psi", 0, 480), R("pu", 0, 30)), col(5), None, A.add)
     for k in range(5):
         for b in range(4):
@@ -270,65 +284,32 @@ def rank_program(g, core, T, topo):
     asel(R("e2", 0, 512), R("e1", 0, 512), [[-16, 8], [0, 64]], A.is_ge, 0, 1)
     for w in range(4):
         asel(R("ew", 512 * w, 512 * w + 512), R("e2", 0, 512), [[0, 8], [1, 4], [0, 16]], A.is_equal, -w, 0)
-    const("zpad", 0, 512, 0)
-    for c0, c1, x in ((0, 30, -1024), (30, 60, 2560), (60, 96, 3584)):
-        const("kp", c0, c1, x)
-    const("kt", 0, 24, -1024)
-    const("kt", 24, 30, 1280)
-    const("actt", 0, 30, 1)
+    const("loc1", 0, 4096, 0)
     for k in range(8):
         const("yw", BLK * k + 1920, BLK * k + 2048, 0)
     for b in range(4):
         asel(R("ed", 512 * b, 512 * b + 512), R("ones", 0, 512), [[1, 512]], A.is_equal, -b, -4)
-    iota(R("opw", 0, 3840), [[1, 3840]])
 
-    def prepare(m, a1, a2, a3, v1, v3, k0):
-        tt(R("src", 0, 384), ind(R("j5", 0, 384), lst(a1)), R("ji", 0, 384), A.add)
-        scatter("r2" + m, 384, lst(a2), "src")
-        tt(R("src", 0, 384), ind(R(v1, 0, 384), lst(a2)), R("l2h", 0, 384), A.add)
-        scatter("r3" + m, 384, lst(a3), "src")
-        tt(R("lcd", 0, 24), lst(a3, "li"), lst(a2, "li"), A.subtract)
-        X("lcd:0:24 lcd:0:24 * #10")
-        tt(R("lc" + m, 0, 24), R("lcd", 0, 24), lst(a2, "li"), A.add)
-        X("lcu$:0:24 lc$:0:24", m)
-        ql, fb = R("qlu", 0, 6), "fb" + m
-        act(R(fb, 0, 384), R("ji", 0, 384))
-        for c0, c1, w, off in ((384, 480, v3, ql), (480, 864, "r2" + m, lst(a3)), (864, 960, "r2" + m, ql),
-                               (960, 1344, v1, R("lcu" + m, 0, 24)), (1344, 1440, v1, ql), (1440, 1536, "r3" + m, ql)):
-            act(R(fb, c0, c1), ind(R(w, 0, 384), off))
-        act(R("ft" + m, 0, 1536), ind(R(fb, 0, 1536), R("sgu", 0, 96)))
-        turn("ft" + m, k0)
-        turn(fb, k0 + 96)
-
-    def tables(m, a1, k0):
-        turned(k0)
-        X("bli:0:96 trd:%d:%d" % (k0, k0 + 96))
-        turned(k0 + 96)
-        X("tb:0:72 trd:%d:%d" % (k0 + 120, k0 + 192))
-        cp(R("lnn", 0, 24), lst(a1, "li"))
-        X("""blm:0:96 bli:0:96 & 511
-        tlo:0:72 tb:0:72 & 511
-        thi:0:72 tb:0:72 >> 9
-        lnn:60:84 lc$:0:24
-        lnn:84:90 qlf:0:6
-        blu$:0:96 blm:0:96
-        t96$:0:24 jst:0:24
-        t96$:24:96 tlo:0:72 + #3
-        lnn:24:30 thi:66:72
-        lnn:30:60 thi:6:36
-        t96$:24:30 t96$:24:30 + 1024.0
-        t96$:30:60 t96$:30:60 + 512.0
-        l3:0:90 lnn:0:90 & 3
-        l4:0:90 lnn:0:90 >> 2
-        l5:0:90 l3:0:90 * 1024.0 + #14
-        t90$:0:90 l5:0:90 + l4:0:90""", m)
-
-    prepare("F", 1, 2, 3, "i1", "i3", 0)
+    tt(R("src", 0, 384), ind(R("j5", 0, 384), lst(1)), JI, A.add)
+    scatter("r2", 384, lst(2), R("src", 0, 384))
+    tt(R("src", 0, 384), ind(R("i1", 0, 384), lst(2)), R("l2h", 0, 384), A.add)
+    scatter("r3", 384, lst(3), R("src", 0, 384))
+    X("""lcd:0:24 li:48:72 - li:24:48
+    lcd:0:24 lcd:0:24 * #10
+    lc:0:24 lcd:0:24 + li:24:48
+    lcu:0:24 lc:0:24""")
+    ql = R("qlu", 0, 6)
+    act(R("fb", 0, 384), JI)
+    for c0, c1, w, off in ((384, 480, "i3", ql), (480, 864, "r2", lst(3)), (864, 960, "r2", ql),
+                           (960, 1344, "i1", R("lcu", 0, 24)), (1344, 1440, "i1", ql), (1440, 1536, "r3", ql)):
+        act(R("fb", c0, c1), ind(R(w, 0, 384), off))
+    act(R("ft", 0, 1536), ind(R("fb", 0, 1536), R("sgu", 0, 96)))
+    turn("fb", 96)
+    turn("ft", 0)
     rotate("yw", BLK, 0, 1920, "s")
     rotate("loc0", 512, 0, 512, "s")
     dmas([("s", codes("qw", 0, 512, dt.uint8), ext(T.wc[:, :])), ("s", R("sw", 0, 512), ext(T.ws[:, :]))])
     dmas([("s", R("vt", 0, 512), ext(T.v[:, :]))])
-    prepare("B", 3, 2, 1, "i3", "i1", 192)
     for dst, c0, n, oh, add in ((12, 16, 16, "ohq", 0.0), (7, 0, 8, "oh", -1.0), (9, 8, 8, "oh", 99.0)):
         o, i = col(dst), R("pr", 0, n)
         tt(i, R(oh, 0, n), R("cf", c0, c0 + n), A.mult)
@@ -338,54 +319,65 @@ def rank_program(g, core, T, topo):
     act(R("eb", 0, 2048), R("ew", 0, 2048), "Identity", col(12))
     X("""#8 #1 >= 4.0 * -2.0
     sc:15:16 oh:1:2 + oh:6:7
-    #13 pid:7:8 * -1.0 + 1.0
     pid:2:3 pid:0:1 >> 1 & 3
     #8 #8 + 1.0
     #11 #15 * -1.0 + 1.0
-    #13 sc:13:14 - ohq:6:7""")
-    for m, sgn, a6, a16 in (("F", "16.0 + 0.0", "-15.0", "-16.0"), ("B", "-16.0 + 32.0", "17.0", "16.0")):
-        X("""#17 pid:2:3 * %s
-        #18 ohq:6:7 * %s
-        #20 ohq:6:7 * %s
-        #17 sc:17:18 + pid:7:8
-        #17 sc:17:18 + sc:18:19
-        ulf:0:8 k16:0:8 * 0.0 + #17
-        ulf:1:2 ulf:1:2 + sc:20:21
-        ulf:6:7 ulf:6:7 + sc:20:21
-        ulu$:0:8 ulf:0:8""" % (sgn, a6, a16), m)
+    #18 ohq:6:7 * -15.0
+    #17 pid:2:3 * 16.0
+    #20 ohq:6:7 * -16.0
+    #18 sc:18:19 + pid:7:8
+    #17 sc:17:18 + sc:18:19
+    ulf:0:8 k16:0:8 * 0.0 + #17
+    ulf:1:2 ulf:1:2 + sc:20:21
+    ulf:6:7 ulf:6:7 + sc:20:21
+    ulu:0:8 ulf:0:8""")
     quant("u", 0, 128, "ut")
-    for m in "FB":
-        o, w = codes("qu" + m, 0, 128, dt.uint32), ind(codes("qu", 0, 128, dt.uint32), R("ulu" + m, 0, 8))
-        emit("v", lambda: g.vector.tensor_copy(o[0], w[0]), w[1], o[1])
-        cp(R("su" + m, 0, 128), ind(R("su", 0, 128), R("ulu" + m, 0, 8)))
+    o, w = codes("qup", 0, 128, dt.uint32), ind(codes("qu", 0, 128, dt.uint32), R("ulu", 0, 8))
+    emit("v", lambda: g.vector.tensor_copy(o[0], w[0]), w[1], o[1])
+    cp(R("sup", 0, 128), ind(R("su", 0, 128), R("ulu", 0, 8)))
     quant("x", 0, 384, "xin")
     X("""actt:0:24 actt:0:24 * #11
     qq:84:90 k16:0:6 * 0.0 + #6
     qq:84:90 qq:84:90 * 512.0""")
     quant("b", 384, 512, "zpad")
-    scatter("frb", 480, R("pu", 0, 30), "ji")
+    scatter("frb", 480, R("pu", 0, 30), R("ji", 0, 480))
     X("fm:0:480 frb:0:480 * mk:0:480")
     scan(480, "fm")
     X("plu:0:30 scn:15:480:16")
-    tables("F", 1, 0)
+    turned(96)
+    X("""tb:0:72 trd:120:192
+    lnn:0:24 li:0:24
+    lnn:60:84 lc:0:24
+    tlo:0:72 tb:0:72 & 511
+    thi:0:72 tb:0:72 >> 9
+    lnn:84:90 qlf:0:6
+    t96:0:24 jst:0:24
+    t96:24:96 tlo:0:72 + #3
+    lnn:24:30 thi:66:72
+    lnn:30:60 thi:6:36
+    t96:24:30 t96:24:30 + 1024.0
+    t96:30:60 t96:30:60 + 512.0
+    l3:0:90 lnn:0:90 & 3
+    l4:0:90 lnn:0:90 >> 2
+    l5:0:90 l3:0:90 * 1024.0 + #14
+    t90:0:90 l5:0:90 + l4:0:90""")
     for w in range(4):
         quant("e", 128 * w, 128 * w + 128, "eb", 512 * w)
+    turned(0)
+    X("""bli:0:96 trd:0:96
+    blm:0:96 bli:0:96 & 511
+    blu:0:96 blm:0:96""")
 
-    def bits(m):
-        mm(0, 384, "u" + m, 0, "x", 0)
-        bw, s = R("bw" + m, 0, 384), R(BANKS[0], 0, 384)
-        if m == "F":
-            ts(bw, s, 0.0, None, A.is_gt)
-        else:
-            ts(bw, s, 0.0, col(13), A.is_gt, A.not_equal)
-        act(R("bt", 768, 1536), ind(bw, R("blu" + m, 48, 96)))
-        cp(R("bt", 0, 768), ind(bw, R("blu" + m, 0, 48)))
+    def moves():
+        mm(0, 384, "up", 0, "x", 0)
+        bw = R("bw", 0, 384)
+        ts(bw, R(BANKS[0], 0, 384), 0.0, None, A.is_gt)
+        act(R("bt", 768, 1536), ind(bw, R("blu", 48, 96)))
+        cp(R("bt", 0, 768), ind(bw, R("blu", 0, 48)))
         quant("b", 0, 384, "bt")
         for w in range(4):
             mm(1, 128, "e", 128 * w, "b", 96 * w, w == 0, w == 3)
         cp(R("cv", 0, 96), R(BANKS[1], 0, 96))
-
-    def origins(m):
         X("""p1:0:96 cv:0:96 & 1
         qq:0:24 cv:0:24 & 512
         qq:24:30 cv:24:30 >> 1 & 512
@@ -395,8 +387,8 @@ def rank_program(g, core, T, topo):
         p2:0:60 cv:0:60 >> 2 & 1
         p3:0:30 cv:0:30 >> 4 & 1
         b1:0:36 cv:60:96 & 512
-        qt:0:90 qq:0:90 + t90$:0:90
-        pt:0:96 pt:0:96 + t96$:0:96
+        qt:0:90 qq:0:90 + t90:0:90
+        pt:0:96 pt:0:96 + t96:0:96
         ss:0:30 p2:0:30 + p3:0:30
         b2:0:30 cv:30:60 >> 1 & 512
         md:0:6 b1:30:36 = qq:24:30
@@ -426,7 +418,7 @@ def rank_program(g, core, T, topo):
         df:0:30 df:0:30 * ov:0:30
         idi:0:30 df:0:30 + ee:0:30
         idm:0:30 idi:0:30 & 4095
-        flu$:0:30 idm:0:30""", m)
+        flu:0:30 idm:0:30""")
 
     def pick(dst, win, width, off):
         act(R(dst, 224, 480), ind(R(win, 0, width), R(off, 14, 30)))
@@ -459,10 +451,12 @@ def rank_program(g, core, T, topo):
     ne = bin(engs).count("1")
 
     for r in range(3):
-        last = r == 2
-        bits("F")
-        origins("F")
-        pick("fr", "loc%d" % r, 4096, "fluF")
+        last, loc = r == 2, "loc%d" % (r + 1)
+        moves()
+        scatter(loc, 4096, R("flu", 0, 30), R("loc0", 0, 480))
+        gather_home(loc, 4)
+        gather_home(loc, 2)
+        pick("fr", "loc%d" % r, 4096, "flu")
         by_column("fr", "zlu")
         collect("zt", "zlu", 0, 12)
         quant("z", 0, KX, "zt")
@@ -474,6 +468,12 @@ def rank_program(g, core, T, topo):
             hist[kind + "l%d" % r] = [(0, KX, (1, 0), 0, 128, True, "g", "rc%d" % r, 2 * ne, True)]
         cnt["ls%d" % r] = 2 * ne
         cnt["rc%d" % r] = 2 * ne
+        gather_home(loc, 1)
+        if r == 0:
+            const("loc2", 0, 4096, 0)
+        elif r == 1:
+            const("loc3", 0, 4096, 0)
+            iota(R("opw", 0, 3840), [[1, 3840]])
         collect("zt", "zlu", 12, 30)
         quant("z", KX, C, "zt", 4 * KX)
         if r == 0:
@@ -481,27 +481,9 @@ def rank_program(g, core, T, topo):
                 quant("d", 128 * b, 128 * b + 128, "ed", 512 * b)
         layer("z", KX, C - KX, 2)
         rotate("yw", BLK, 768, 1920, "s")
-        if r > 0:
-            bits("B")
-        layer("l%d" % r, 0, KX, 0)
-        rotate("yw", BLK, 0, 768, "sa")
-        if r == 0:
-            tables("B", 3, 192)
-            bits("B")
-        origins("B")
-        loc = "frb" if last else "loc%d" % (r + 1)
-        pick(loc, "loc0", 4096, "fluB")
-        by_column(loc, "xlu")
         if last:
             quant("v", 0, 128, "vt")
-            collect("xt", "xlu", 0, 30)
-            quant("x", 0, 480, "xt")
-            mm(0, 480, "v", 0, "x", 0)
-            act(R("yo", 0, 480), R(BANKS[0], 0, 480))
-            dmas([("s", ext(T.oc[:, :]), codes("qx", 0, 480, dt.uint8))]
-                 + [("s", ext(T.osc[4 * k:4 * k + 4, :]), R("sx", 0, 480, 1, 32 * k, 32 * k + 4)) for k in range(4)])
-            dmas([("a", ext(T.y[:, :]), R("yo", 0, 480))])
-            pick("fr", "loc0", 4096, "fluF")
+            pick("fr", "loc0", 4096, "flu")
             fold("fr")
             X("""cv:0:30 scn:15:480:16
             p1:0:30 cv:0:30 >> 7 & 15
@@ -514,8 +496,20 @@ def rank_program(g, core, T, topo):
             ss:0:30 p1:60:90 * -288.0
             ee:0:30 ee:0:30 + ss:0:30
             zlu:0:30 ee:0:30""")
+        layer("l%d" % r, 0, KX, 0)
+        rotate("yw", BLK, 0, 768, "sa")
+        if last:
             pick("opo", "opw", 3840, "zlu")
             dmas([("s", ext(T.op[k:k + 1, :]), R("opo", 0, 480, 1, 16 * k, 16 * k + 1)) for k in range(8)])
+        by_column(loc, "xlu")
+        if last:
+            collect("xt", "xlu", 0, 30)
+            quant("x", 0, 480, "xt")
+            mm(0, 480, "v", 0, "x", 0)
+            act(R("yo", 0, 480), R(BANKS[0], 0, 480))
+            dmas([("s", ext(T.oc[:, :]), codes("qx", 0, 480, dt.uint8))]
+                 + [("s", ext(T.osc[4 * k:4 * k + 4, :]), R("sx", 0, 480, 1, 32 * k, 32 * k + 4)) for k in range(4)])
+            dmas([("a", ext(T.y[:, :]), R("yo", 0, 480))])
         else:
             rotate(loc, 512, 0, 512, "s")
             collect("xt", "xlu", 0, 24)

from concourse.mybir import dt, AluOpType, AxisListType, ActivationFunctionType

A = AluOpType
OPS = {"+": A.add, "-": A.subtract, "*": A.mult, "&": A.bitwise_and, ">>": A.logical_shift_right, "=": A.is_equal, "!=": A.not_equal, "<": A.is_lt, ">=": A.is_ge, ">": A.is_gt}
MATES = (1, 2, 3)
WEIGHTS = (1, 512, 4, 1024, 16, 2048, 4096)
C, KX = 480, 192
BLK = 2048

SCRATCH, POOL = {}, {}
for _d, _l in (("bfloat16", "xin 1920 xt 1920 zt 1920 yw 16384 ut 512 vt 512 zpad 512 ones 512 mk 480 e0 512 e1 512 e2 512 ew 2048 eb 2048 ed 2048 bw 384 bt 1536 n16 480"),
               ("int32", "pi 30 li 72 pid 8"),
               ("float32", "ji 480 j5 384 psi 480 tr 192 trd 192 rs1 480 i1 384 i3 384 r2 384 r3 384 l2h 384 src 384 fb 1536 ft 1536 fm 480 scn 480 loc0 4096 loc1 4096 loc2 4096 loc3 4096 fr 480 frb 480 opw 3840 opo 480 rb0 288 rb1 288 rb2 288 rb3 288 yo 480")):
    _l = _l.split()
    for _k in range(0, len(_l), 2):
        SCRATCH[_l[_k]] = ("sbuf", [128, int(_l[_k + 1])], _d)
for _b, _d, _l in (
        ("wi", "int32", "lcd 24 lc 24 qli 6 sgi 96 bli 96 blm 96 tb 72 tlo 72 thi 72 lnn 90 l3 90 l4 90 cv 96 p1 96 p2 60 p3 30 b1 36 b2 30 b3 6 qq 90 v21 24 v20 24 idi 30 idm 30"),
        ("wf", "float32", "qlf 6 sgf 96 jst 24 l5 90 t96 96 t90 90 kp 96 kt 30 actt 30 pt 96 qt 90 ss 30 m90 90 mb 30 ov 30 md 6 dd 6 df 90 ee 30"),
        ("wu", "uint16", "pu 30 lu 72 lcu 24 qlu 6 sgu 96 plu 30 blu 96 ulu 8 flu 30 zlu 30 xlu 30"),
        ("cs", "float32", "sc 32 k16 16 oh 8 ohq 16 cf 32 pr 16 ulf 8")):
    _l, _o = _l.split(), 0
    for _k in range(0, len(_l), 2):
        POOL[_l[_k]] = (_b, _o)
        _o += (int(_l[_k + 1]) + 15) // 16 * 16
    SCRATCH[_b] = ("sbuf", [128, _o], _d)
for _n, _w in (("u", 128), ("up", 128), ("v", 128), ("w", 512), ("e", 512), ("d", 512), ("x", 480), ("z", 480), ("b", 512),
               ("l0", KX), ("l1", KX), ("l2", KX)):
    SCRATCH["q" + _n] = ("sbuf", [128, _w], "float8_e4m3fn_x4")
    SCRATCH["s" + _n] = ("sbuf", [128, _w], "uint8")
BANKS = ["bank%d" % _k for _k in range(8)]
for _n in BANKS:
    SCRATCH[_n] = ("psum", [128, 512], "float32")
SEMAPHORES = ["e_v", "e_a", "e_t", "e_g"] + ["d%d" % _k for _k in range(34)] + ["rc%d" % _k for _k in range(3)] + ["ls%d" % _k for _k in range(3)]


def rank_program(g, core, T, topo):
    rank = T.rank_of(core)
    if rank is None:
        return
    ENG = {"v": g.vector, "a": g.scalar, "t": g.tensor, "g": g, "s": g.sync}
    cnt, seen, hist, nb = {}, {q: {} for q in ENG}, {}, [0]

    def R(name, c0, c1, step=1, p0=0, p1=128):
        if name in POOL:
            name, o = POOL[name]
            c0, c1 = c0 + o, c1 + o
        ap = T[name][p0:p1, c0:c1] if step == 1 else T[name][p0:p1, c0:c1:step]
        if name in BANKS:
            return ap, [(name, 0, 512, (1, 0), 0, 128)]
        return ap, [(name, c0, c1, (step, c0 % step), p0, p1)]

    def ind(win, off):
        return win[0].indirect(off[0]), win[1] + off[1]

    def codes(name, c0, c1, d=None):
        ap = T[name][:, c0:c1]
        return (ap if d is None else ap.bitcast(d)), [(name, c0, c1, (1, 0), 0, 128)]

    def emit(q, fn, reads, writes, tok=None):
        dma, need, new = tok is not None, {}, []
        for isw, regs in ((False, reads), (True, writes)):
            for (name, c0, c1, ph, p0, p1) in regs:
                for h in hist.get(name, ()):
                    if h[1] <= c0 or c1 <= h[0] or h[4] <= p0 or p1 <= h[3]:
                        continue
                    if h[2][0] == ph[0] and h[2][1] != ph[1]:
                        continue
                    if q == "t" and h[6] == q and isw:
                        continue
                    if not (isw or h[5] or (name in BANKS and h[6] != q)):
                        continue
                    if dma and tok[0] == h[7]:
                        continue
                    need[h[7]] = max(need.get(h[7], 0), h[8])
                new.append((name, c0, c1, ph, p0, p1, isw))
        for s in need:
            if seen[q].get(s, 0) < need[s]:
                ENG[q].wait_ge(T.sem[s], need[s])
                seen[q][s] = need[s]
        ins = fn()
        if not dma:
            s = "e_" + q
            cnt[s] = cnt.get(s, 0) + 1
            ins.then_inc(T.sem[s], 1)
            tok = (s, cnt[s])
        for (name, c0, c1, ph, p0, p1, isw) in new:
            old = hist.get(name, [])
            if isw and ph[0] == 1:
                old = [h for h in old if not (c0 <= h[0] and h[1] <= c1 and p0 <= h[3] and h[4] <= p1)]
            elif not isw and not dma:
                old = [h for h in old if h[5] or h[9] or h[6] != q or h[:5] != (c0, c1, ph, p0, p1)]
            hist[name] = old + [(c0, c1, ph, p0, p1, isw, q, tok[0], tok[1], dma)]

    def sr(*xs):
        r = []
        for x in xs:
            if isinstance(x, tuple):
                r = r + x[1]
        return r

    def ap(x):
        return x[0] if isinstance(x, tuple) else x

    def col(k):
        return R("sc", k, k + 1)

    def tt(o, a, b, op):
        emit("v", lambda: g.vector.tensor_tensor(o[0], a[0], b[0], op), sr(a, b), o[1])

    def ts(o, a, s1, s2, op0, op1=None):
        if op1 is None:
            emit("v", lambda: g.vector.tensor_scalar(o[0], a[0], ap(s1), None, op0), sr(a, s1), o[1])
        else:
            emit("v", lambda: g.vector.tensor_scalar(o[0], a[0], ap(s1), ap(s2), op0, op1), sr(a, s1, s2), o[1])

    def cp(o, a):
        emit("v", lambda: g.vector.tensor_copy(o[0], a[0]), a[1], o[1])

    def opd(w):
        if w[0] == "#":
            return col(int(w[1:]))
        if ":" in w:
            n, k = w.split(":")[0], [int(z) for z in w.split(":")[1:]]
            return R(n, *k)
        return float(w) if "." in w else int(w)

    def X(text):
        for ln in text.split("\n"):
            w = ln.split()
            if not w:
                continue
            o, a = opd(w[0]), opd(w[1])
            if len(w) == 2:
                cp(o, a)
            elif len(w) == 4 and ":" in w[3]:
                tt(o, a, opd(w[3]), OPS[w[2]])
            elif len(w) == 4:
                ts(o, a, opd(w[3]), None, OPS[w[2]])
            else:
                ts(o, a, opd(w[3]), opd(w[5]), OPS[w[2]], OPS[w[4]])

    def scatter(dst, n, off, i):
        w = ind(R(dst, 0, n), off)
        emit("v", lambda: g.vector.tensor_copy(w[0], i[0]), i[1] + off[1], R(dst, 0, n)[1])

    def act(o, a, func="Copy", scale=1.0):
        if func == "Copy":
            emit("a", lambda: g.scalar.activation(o[0], a[0], ActivationFunctionType.Copy), a[1], o[1])
        else:
            f = ActivationFunctionType.Relu if func == "Relu" else ActivationFunctionType.Identity
            emit("a", lambda: g.scalar.activation(o[0], a[0], f, scale=ap(scale)), sr(a, scale), o[1])

    def quant(x, c0, c1, tile, t0=0):
        q, s, i = codes("q" + x, c0, c1), R("s" + x, c0, c1), R(tile, t0, t0 + 4 * (c1 - c0))
        emit("v", lambda: g.vector.quantize_mx(q[0], s[0], i[0]), i[1], q[1] + s[1])

    def mm(bank, n, a, a0, b, b0, start=True, stop=True):
        o, la, sa, lb, sb = R(BANKS[bank], 0, n), codes("q" + a, a0, a0 + 128), R("s" + a, a0, a0 + 128), codes("q" + b, b0, b0 + n), R("s" + b, b0, b0 + n)
        emit("t", lambda: g.tensor.matmul_mx(o[0], la[0], sa[0], lb[0], sb[0], start, stop), sr(la, sa, lb, sb), o[1])

    def iota(o, pat, fl=True, cm=0, base=0):
        if fl:
            emit("g", lambda: g.iota(o[0], pat, base, cm, allow_small_or_imprecise_dtypes=True), [], o[1])
        else:
            emit("g", lambda: g.iota(o[0], pat, base, cm), [], o[1])

    def const(name, c0, c1, val):
        iota(R(name, c0, c1), [[0, c1 - c0]], True, 0, val)

    def asel(o, a, pat, op, base, cm):
        emit("g", lambda: g.affine_select(o[0], a[0], pat, op, 0.0, base, cm), a[1], o[1])

    def batch(n):
        s = "d%d" % nb[0]
        nb[0] += 1
        cnt[s] = 16 * n
        return s, 16 * n

    def dmas(items):
        t = batch(len(items))
        for q, o, i in items:
            emit(q, lambda: ENG[q].dma_start(o[0], i[0]).then_inc(T.sem[t[0]], 16), i[1], o[1], t)

    def ext(a):
        return a, []

    def turn(src, k0):
        dmas([("s", R("tr", k0 + 32 * b + 16 * (k % 2), k0 + 32 * b + 16 * (k % 2) + 16, 1, 32 * (k // 2), 32 * (k // 2) + 32),
               R(src, 512 * b, 512 * b + 512, 1, 16 * k, 16 * k + 1)) for k in range(8) for b in range(3)])

    def turned(k0):
        o, i = R("trd", k0, k0 + 96), R("tr", k0, k0 + 96)
        emit("v", lambda: g.vector.transpose(o[0], i[0]), i[1], o[1])

    def scan(n, src):
        o, d0, d1 = R("scn", 0, n), R("rs1", 0, n), R(src, 0, n)
        emit("v", lambda: g.vector.tensor_tensor_scan(o[0], d0[0], d1[0], 0.0, A.mult, A.add), sr(d0, d1), o[1])

    def rotate(name, blk, c0, c1, qs):
        it = []
        for k in range(1, 8):
            e = 128 - 16 * k
            it.append((blk * k, 0, e, 16 * k, 128))
            it.append((blk * k, e, 128, 0, 16 * k))
        dmas([(qs[n % len(qs)], R(name, o + c0, o + c1, 1, a, b), R(name, c0, c1, 1, d, e)) for n, (o, a, b, d, e) in enumerate(it)])

    def gather_home(name, s):
        t, w, e = batch(2), 512 * s, 128 - 16 * s
        for a, b, c, d in ((16 * s, 128, 0, e), (0, 16 * s, e, 128)):
            o, i = R(name, 0, w, 1, a, b), R(name, w, 2 * w, 1, c, d)
            emit("g", lambda: g.dma_start(o[0], i[0], accum_op=A.add).then_inc(T.sem[t[0]], 16), i[1], o[1], t)

    dmas([("s" if k % 2 else "a", R("li", 0, 72, 1, 16 * k, 16 * k + 16), ext(T.ln[:, :])) for k in range(8)])
    dmas([("s", R("xin", 0, 1920), ext(T.x[:, :]))])
    dmas([("a", R("pi", 0, 30), ext(T.p[:, :])), ("a", R("ut", 0, 512), ext(T.u[:, :]))])

    iota(R("pid", 0, 1), [[1, 1]], False, 1)
    iota(R("k16", 0, 16), [[1, 16]])
    iota(R("ji", 0, 480), [[1, 480]])
    iota(R("psi", 0, 480), [[384, 5], [1, 96]])
    iota(R("qli", 0, 6), [[64, 6]], False)
    iota(R("sgi", 0, 96), [[4, 4], [64, 24]], False)
    iota(R("jst", 0, 24), [[16, 24]])
    iota(R("n16", 0, 480), [[0, 30], [1, 16]])
    const("cf", 0, 32, 0)
    for k, x in ((0, 6), (2, 22), (5, 1), (7, 17), (8, -83), (9, -79), (14, -99), (15, -103)) + tuple((16 + k, WEIGHTS[k]) for k in range(7)):
        const("cf", k, k + 1, x)
    const("ones", 0, 512, 1)
    const("zpad", 0, 512, 0)
    for c0, c1, x in ((0, 30, -1024), (30, 60, 2560), (60, 96, 3584)):
        const("kp", c0, c1, x)
    const("kt", 0, 24, -1024)
    const("kt", 24, 30, 1280)
    const("actt", 0, 30, 1)
    X("""pid:1:2 pid:0:1 & 15
    pid:2:3 pid:0:1 >> 4
    pid:3:4 pid:0:1 >> 2 & 3
    pid:4:5 pid:0:1 & 3
    pid:5:6 pid:0:1 >> 4 & 1
    pid:6:7 pid:0:1 >> 5
    pid:7:8 pid:0:1 & 1
    #0 pid:1:2
    #1 pid:2:3
    #3 pid:2:3 * -512.0
    #4 pid:2:3 * -2048.0
    #5 pid:2:3 * 2048.0
    #6 pid:5:6
    #2 pid:3:4 * 16.0
    #19 pid:1:2 * 4.0
    #16 pid:6:7
    oh:0:8 k16:0:8 = #1
    ohq:0:16 k16:0:16 = #0
    #2 sc:2:3 + pid:4:5
    #14 #3 + 384.0
    #10 oh:0:1 + oh:7:8
    #19 sc:19:20 + sc:16:17""")

    def lst(i, buf="lu"):
        return R(buf, 24 * i - 24, 24 * i)

    JI = R("ji", 0, 384)
    X("lu:0:72 li:0:72")
    scatter("i1", 384, lst(1), JI)
    scatter("i3", 384, lst(3), JI)
    X("""j5:0:384 ji:0:384 * 512.0
    pu:0:30 pi:0:30
    mk:0:480 n16:0:480 = #0
    rs1:0:480 n16:0:480 > 0.0""")
    const("loc0", 480, 512, 0)
    ts(R("loc0", 0, 480), ind(R("psi", 0, 480), R("pu", 0, 30)), col(5), None, A.add)
    for k in range(5):
        for b in range(4):
            act(R("yw", 384 * k + 96 * b, 384 * k + 96 * b + 96), R("xin", 384 * k + b, 384 * k + 384, 4))
    act(R("l2h", 0, 384), ind(R("j5", 0, 384), lst(2)))
    X("""qlf:0:6 qli:0:6 + #19
    sgf:0:96 sgi:0:96 + #2
    jst:0:24 jst:0:24 + #0 + 1536.0
    qlu:0:6 qlf:0:6
    sgu:0:96 sgf:0:96""")

    asel(R("e0", 0, 512), R("ones", 0, 512), [[0, 32], [1, 4], [-1, 4]], A.is_equal, 0, 0)
    asel(R("e1", 0, 512), R("e0", 0, 512), [[16, 8], [0, 64]], A.is_ge, 15, -1)
    asel(R("e2", 0, 512), R("e1", 0, 512), [[-16, 8], [0, 64]], A.is_ge, 0, 1)
    for w in range(4):
        asel(R("ew", 512 * w, 512 * w + 512), R("e2", 0, 512), [[0, 8], [1, 4], [0, 16]], A.is_equal, -w, 0)
    const("loc1", 0, 4096, 0)
    for k in range(8):
        const("yw", BLK * k + 1920, BLK * k + 2048, 0)
    for b in range(4):
        asel(R("ed", 512 * b, 512 * b + 512), R("ones", 0, 512), [[1, 512]], A.is_equal, -b, -4)

    tt(R("src", 0, 384), ind(R("j5", 0, 384), lst(1)), JI, A.add)
    scatter("r2", 384, lst(2), R("src", 0, 384))
    tt(R("src", 0, 384), ind(R("i1", 0, 384), lst(2)), R("l2h", 0, 384), A.add)
    scatter("r3", 384, lst(3), R("src", 0, 384))
    X("""lcd:0:24 li:48:72 - li:24:48
    lcd:0:24 lcd:0:24 * #10
    lc:0:24 lcd:0:24 + li:24:48
    lcu:0:24 lc:0:24""")
    ql = R("qlu", 0, 6)
    act(R("fb", 0, 384), JI)
    for c0, c1, w, off in ((384, 480, "i3", ql), (480, 864, "r2", lst(3)), (864, 960, "r2", ql),
                           (960, 1344, "i1", R("lcu", 0, 24)), (1344, 1440, "i1", ql), (1440, 1536, "r3", ql)):
        act(R("fb", c0, c1), ind(R(w, 0, 384), off))
    act(R("ft", 0, 1536), ind(R("fb", 0, 1536), R("sgu", 0, 96)))
    turn("fb", 96)
    turn("ft", 0)
    rotate("yw", BLK, 0, 1920, "s")
    rotate("loc0", 512, 0, 512, "s")
    dmas([("s", codes("qw", 0, 512, dt.uint8), ext(T.wc[:, :])), ("s", R("sw", 0, 512), ext(T.ws[:, :]))])
    dmas([("s", R("vt", 0, 512), ext(T.v[:, :]))])
    for dst, c0, n, oh, add in ((12, 16, 16, "ohq", 0.0), (7, 0, 8, "oh", -1.0), (9, 8, 8, "oh", 99.0)):
        o, i = col(dst), R("pr", 0, n)
        tt(i, R(oh, 0, n), R("cf", c0, c0 + n), A.mult)
        emit("v", lambda: g.vector.tensor_reduce(o[0], i[0], AxisListType.X, A.add), i[1], o[1])
        if add:
            ts(col(dst), col(dst), add, None, A.add)
    act(R("eb", 0, 2048), R("ew", 0, 2048), "Identity", col(12))
    X("""#8 #1 >= 4.0 * -2.0
    sc:15:16 oh:1:2 + oh:6:7
    pid:2:3 pid:0:1 >> 1 & 3
    #8 #8 + 1.0
    #11 #15 * -1.0 + 1.0
    #18 ohq:6:7 * -15.0
    #17 pid:2:3 * 16.0
    #20 ohq:6:7 * -16.0
    #18 sc:18:19 + pid:7:8
    #17 sc:17:18 + sc:18:19
    ulf:0:8 k16:0:8 * 0.0 + #17
    ulf:1:2 ulf:1:2 + sc:20:21
    ulf:6:7 ulf:6:7 + sc:20:21
    ulu:0:8 ulf:0:8""")
    quant("u", 0, 128, "ut")
    o, w = codes("qup", 0, 128, dt.uint32), ind(codes("qu", 0, 128, dt.uint32), R("ulu", 0, 8))
    emit("v", lambda: g.vector.tensor_copy(o[0], w[0]), w[1], o[1])
    cp(R("sup", 0, 128), ind(R("su", 0, 128), R("ulu", 0, 8)))
    quant("x", 0, 384, "xin")
    X("""actt:0:24 actt:0:24 * #11
    qq:84:90 k16:0:6 * 0.0 + #6
    qq:84:90 qq:84:90 * 512.0""")
    quant("b", 384, 512, "zpad")
    scatter("frb", 480, R("pu", 0, 30), R("ji", 0, 480))
    X("fm:0:480 frb:0:480 * mk:0:480")
    scan(480, "fm")
    X("plu:0:30 scn:15:480:16")
    turned(96)
    X("""tb:0:72 trd:120:192
    lnn:0:24 li:0:24
    lnn:60:84 lc:0:24
    tlo:0:72 tb:0:72 & 511
    thi:0:72 tb:0:72 >> 9
    lnn:84:90 qlf:0:6
    t96:0:24 jst:0:24
    t96:24:96 tlo:0:72 + #3
    lnn:24:30 thi:66:72
    lnn:30:60 thi:6:36
    t96:24:30 t96:24:30 + 1024.0
    t96:30:60 t96:30:60 + 512.0
    l3:0:90 lnn:0:90 & 3
    l4:0:90 lnn:0:90 >> 2
    l5:0:90 l3:0:90 * 1024.0 + #14
    t90:0:90 l5:0:90 + l4:0:90""")
    for w in range(4):
        quant("e", 128 * w, 128 * w + 128, "eb", 512 * w)
    turned(0)
    X("""bli:0:96 trd:0:96
    blm:0:96 bli:0:96 & 511
    blu:0:96 blm:0:96""")

    def moves():
        mm(0, 384, "up", 0, "x", 0)
        bw = R("bw", 0, 384)
        ts(bw, R(BANKS[0], 0, 384), 0.0, None, A.is_gt)
        act(R("bt", 768, 1536), ind(bw, R("blu", 48, 96)))
        cp(R("bt", 0, 768), ind(bw, R("blu", 0, 48)))
        quant("b", 0, 384, "bt")
        for w in range(4):
            mm(1, 128, "e", 128 * w, "b", 96 * w, w == 0, w == 3)
        cp(R("cv", 0, 96), R(BANKS[1], 0, 96))
        X("""p1:0:96 cv:0:96 & 1
        qq:0:24 cv:0:24 & 512
        qq:24:30 cv:24:30 >> 1 & 512
        qq:30:60 cv:30:60 & 512
        qq:60:84 cv:0:24 >> 3 & 512
        pt:0:96 p1:0:96 * kp:0:96
        p2:0:60 cv:0:60 >> 2 & 1
        p3:0:30 cv:0:30 >> 4 & 1
        b1:0:36 cv:60:96 & 512
        qt:0:90 qq:0:90 + t90:0:90
        pt:0:96 pt:0:96 + t96:0:96
        ss:0:30 p2:0:30 + p3:0:30
        b2:0:30 cv:30:60 >> 1 & 512
        md:0:6 b1:30:36 = qq:24:30
        v21:0:24 cv:0:24 & 21
        ss:0:30 ss:0:30 * kt:0:30
        dd:0:6 pt:90:96 - qt:24:30
        m90:24:30 p2:24:30 != p3:24:30
        m90:30:60 p1:30:60 != p2:30:60
        pt:0:30 pt:0:30 + ss:0:30
        dd:0:6 dd:0:6 * md:0:6
        m90:60:90 b1:0:30 != qq:60:90
        m90:0:24 v21:0:24 = #7
        qt:24:30 qt:24:30 + dd:0:6
        v20:0:24 cv:0:24 & 20
        b3:0:6 cv:24:30 >> 2 & 512
        df:0:90 qt:0:90 - pt:0:90
        mb:0:30 b2:0:30 = qq:60:90
        ov:24:30 b3:0:6 = qq:84:90
        df:0:90 df:0:90 * m90:0:90
        mb:0:30 mb:0:30 * actt:0:30
        ov:0:24 v20:0:24 * #8 < #9
        df:0:90 df:0:90 + pt:0:90
        ee:0:30 df:30:60 - df:60:90
        ee:0:30 ee:0:30 * mb:0:30
        ee:0:30 ee:0:30 + df:60:90
        df:0:30 df:0:30 - ee:0:30
        df:0:30 df:0:30 * ov:0:30
        idi:0:30 df:0:30 + ee:0:30
        idm:0:30 idi:0:30 & 4095
        flu:0:30 idm:0:30""")

    def pick(dst, win, width, off):
        act(R(dst, 224, 480), ind(R(win, 0, width), R(off, 14, 30)))
        cp(R(dst, 0, 224), ind(R(win, 0, width), R(off, 0, 14)))

    def fold(src):
        tt(R("fm", 0, 480), ind(R(src, 0, 480), R("plu", 0, 30)), R("mk", 0, 480), A.mult)
        scan(480, "fm")

    def by_column(src, dst):
        fold(src)
        X("idi:0:30 scn:15:480:16 + #4\nidm:0:30 idi:0:30 & %d\n%s:0:30 idm:0:30" % (8 * BLK - 1, dst))

    def collect(tile, off, k0, k1):
        for b in range(4):
            (cp, act)[b % 2](R(tile, 64 * k0 + b, 64 * k1, 4), ind(R("yw", 96 * b, 8 * BLK), R(off, k0, k1)))

    def layer(src, c0, n, i0):
        for b in range(4):
            mm(b, n, "w", 128 * b, src, c0)
            mm(4 + b, n, "d", 128 * b, src, c0)
            act(R("rb%d" % b, 0, n), R(BANKS[b], 0, n), "Relu", 0.015625)
        for b in range(4):
            for k in range(n // 96):
                d = 384 * (i0 + k) + 96 * b
                tt(R("yw", d, d + 96), R("rb%d" % b, 96 * k, 96 * k + 96), R(BANKS[4 + b], 96 * k, 96 * k + 96), A.add)

    peers = [T.cores[rank ^ k] for k in MATES]
    engs = topo.mask(core, peers[0]) & topo.mask(core, peers[1]) & topo.mask(core, peers[2])
    ne = bin(engs).count("1")

    for r in range(3):
        last, loc = r == 2, "loc%d" % (r + 1)
        moves()
        scatter(loc, 4096, R("flu", 0, 30), R("loc0", 0, 480))
        gather_home(loc, 4)
        gather_home(loc, 2)
        pick("fr", "loc%d" % r, 4096, "flu")
        by_column("fr", "zlu")
        collect("zt", "zlu", 0, 12)
        quant("z", 0, KX, "zt")
        rid, pid, _se = topo.addr(peers[r])
        for kind in "qs":
            i = codes("qz", 0, KX, dt.uint8) if kind == "q" else R("sz", 0, KX)
            o = codes("ql%d" % r, 0, KX, dt.uint8) if kind == "q" else R("sl%d" % r, 0, KX)
            emit("g", lambda: g.remote_dma(o[0], i[0], T.sem["rc%d" % r], T.sem["ls%d" % r], pid, rid, engs), i[1], [], ("ls%d" % r, 2 * ne))
            hist[kind + "l%d" % r] = [(0, KX, (1, 0), 0, 128, True, "g", "rc%d" % r, 2 * ne, True)]
        cnt["ls%d" % r] = 2 * ne
        cnt["rc%d" % r] = 2 * ne
        gather_home(loc, 1)
        if r == 0:
            const("loc2", 0, 4096, 0)
        elif r == 1:
            const("loc3", 0, 4096, 0)
            iota(R("opw", 0, 3840), [[1, 3840]])
        collect("zt", "zlu", 12, 30)
        quant("z", KX, C, "zt", 4 * KX)
        if r == 0:
            for b in range(4):
                quant("d", 128 * b, 128 * b + 128, "ed", 512 * b)
        layer("z", KX, C - KX, 2)
        rotate("yw", BLK, 768, 1920, "s")
        if last:
            quant("v", 0, 128, "vt")
            pick("fr", "loc0", 4096, "flu")
            fold("fr")
            X("""cv:0:30 scn:15:480:16
            p1:0:30 cv:0:30 >> 7 & 15
            p2:0:30 cv:0:30 >> 11
            p3:0:30 cv:0:30 & 2047
            p1:30:60 p1:0:30 * 171.0
            ee:0:30 p2:0:30 * 480.0
            p1:60:90 p1:30:60 >> 9
            ee:0:30 ee:0:30 + p3:0:30
            ss:0:30 p1:60:90 * -288.0
            ee:0:30 ee:0:30 + ss:0:30
            zlu:0:30 ee:0:30""")
        layer("l%d" % r, 0, KX, 0)
        rotate("yw", BLK, 0, 768, "sa")
        if last:
            pick("opo", "opw", 3840, "zlu")
            dmas([("s", ext(T.op[k:k + 1, :]), R("opo", 0, 480, 1, 16 * k, 16 * k + 1)) for k in range(8)])
        by_column(loc, "xlu")
        if last:
            collect("xt", "xlu", 0, 30)
            quant("x", 0, 480, "xt")
            mm(0, 480, "v", 0, "x", 0)
            act(R("yo", 0, 480), R(BANKS[0], 0, 480))
            dmas([("s", ext(T.oc[:, :]), codes("qx", 0, 480, dt.uint8))]
                 + [("s", ext(T.osc[4 * k:4 * k + 4, :]), R("sx", 0, 480, 1, 32 * k, 32 * k + 4)) for k in range(4)])
            dmas([("a", ext(T.y[:, :]), R("yo", 0, 480))])
        else:
            rotate(loc, 512, 0, 512, "s")
            collect("xt", "xlu", 0, 24)
            quant("x", 0, 384, "xt")
    for s in sorted(cnt):
        g.wait_ge(T.sem[s], cnt[s])
